import numpy as np
import ml_dtypes


def mxq(x, axis, fmt="e4m3"):
    dtype, down = {"e4m3": (ml_dtypes.float8_e4m3fn, 7), "e5m2": (ml_dtypes.float8_e5m2, 14)}[fmt]
    v = np.moveaxis(np.asarray(x, np.float32).astype(ml_dtypes.bfloat16).astype(np.float64), axis, -1)
    blocks = v.reshape(v.shape[:-1] + (-1, 32))
    amax = np.abs(blocks).max(-1, keepdims=True)
    byte = np.maximum(np.where(amax > 0, np.frexp(amax)[1] - 1 + 127, 0) - down, 1)
    scale = np.exp2(byte - 127.0)
    codes = (blocks / scale).astype(np.float32).astype(dtype).astype(np.float64)
    return np.moveaxis((codes * scale).reshape(v.shape), -1, axis)


WIDE = False


def mx_kscale(k):
    if not WIDE:
        return np.ones(k)
    levels = np.array([18, -18])
    if k % 512:
        return np.exp2(np.random.permutation(np.resize(levels, k // 32))).repeat(32)
    a = np.empty((k // 512, 16))
    for p in range(k // 512):
        a[p, :8] = np.random.permutation(np.resize(levels, 8))
        for g in range(8):
            far = levels[np.abs(levels - a[p, g]) >= 10]
            a[p, g + 8] = far[np.random.randint(len(far))]
    return np.exp2(a.ravel()).repeat(32)


def f64(x):
    return np.asarray(x).astype(np.float64)


def striped(idx):
    return np.tile(np.asarray(idx).reshape(-1, 16).T, (8, 1)).astype(np.uint16)


def unstriped(offs):
    return offs[:16].T.reshape(-1).astype(np.int64)


T, C, D, DV = 512, 1024, 512, 1024
BETA = 0.25


def setup_inputs():
    n = np.random.standard_normal
    grid = lambda v: np.clip(np.round(v * 16) / 16, -4, 4)
    v = mx_kscale(DV)[:, None]
    return {
        "zT": (grid(n((DV, T))) * v).astype(np.float32),
        "cb": (grid(n((DV, C))) * v).astype(np.float32),
        "dyT": (grid(0.5 * n((DV, T))) * v).astype(np.float32),
        "wm": (n((DV, D)) / np.sqrt(DV) / v).astype(np.float32),
        "offs": striped(np.random.randint(0, C, T)),
    }


def reference(zT, cb, dyT, wm, offs):
    e = f64(zT) - f64(cb)[:, unstriped(offs)]
    g = (f64(dyT) + BETA * e)
    return mxq(f64(wm), 0, "e4m3").T @ mxq(g, 0, "e5m2")

@@ -1,0 +1,153 @@
+from contextlib import ExitStack
+
+import concourse.mybir as mybir
+
+T, C, D, DV = 512, 1024, 512, 1024
+BETA = 0.25
+FLOPS = 2 * DV * D * T
+
+F32 = mybir.dt.float32
+BF16 = mybir.dt.bfloat16
+U32 = mybir.dt.uint32
+U16 = mybir.dt.uint16
+U8 = mybir.dt.uint8
+E4M3 = mybir.dt.float8_e4m3fn_x4
+E5M2 = mybir.dt.float8_e5m2_x4
+MULT = mybir.AluOpType.mult
+ADD = mybir.AluOpType.add
+
+P = 128
+PACK = 4
+K_PASS = P * PACK
+PASSES = DV // K_PASS
+HALF = T // 2
+RUN = 2
+
+
+def planar(ap):
+    return ap.rearrange("p j (c i) -> p c j i", i=RUN)
+
+
+def packed(ap):
+    return ap.rearrange("p (c i) j -> p c j i", i=RUN)
+
+
+def tile_attend_gvq_s_x_kernel(tc, zT, cb, dyT, wm, offs, out):
+    nc = tc.nc
+
+    def rows(x, g):
+        return x[g * K_PASS : (g + 1) * K_PASS, :].rearrange("(p j) w -> p j w", j=PACK)
+
+    with ExitStack() as ctx:
+        keep = ctx.enter_context(tc.tile_pool(name="keep", bufs=1))
+        psum = ctx.enter_context(tc.psum_pool(name="psum", bufs=1))
+
+        offsets = keep.tile([P, T // 16], U16, name="offsets")
+        minus_beta = keep.tile([P, T], F32, name="minus_beta")
+        nc.gpsimd.memset(minus_beta[:], -BETA)
+
+        g_codes = keep.tile([P, PASSES, T], U32, name="g_codes", align_bytes=64)
+        g_scales = keep.tile([P, PASSES, T], U8, name="g_scales", align_bytes=64)
+        w_codes = keep.tile([P, PASSES, D], U32, name="w_codes", align_bytes=64)
+        w_scales = keep.tile([P, PASSES, D], U8, name="w_scales", align_bytes=64)
+
+        w_bf = keep.tile([P, PASSES, D, PACK], BF16, name="w_bf", align_bytes=64)
+        banks = [psum.tile([P, T], F32, name="bank%d" % m) for m in range(D // P)]
+        parts = [keep.tile([P, PACK, T], F32, name="part%d" % g, align_bytes=64) for g in range(PASSES)]
+        g_bf = [keep.tile([P, T, PACK], BF16, name="g_bf%d" % g, align_bytes=64) for g in range(PASSES)]
+        halves = [slice(0, HALF), slice(HALF, T)]
+
+        def commitment(g):
+            part = parts[g]
+            for h in range(2):
+                for j in (2 * h, 2 * h + 1):
+                    book = keep.tile([P, C], F32, name="book%d_%d" % (g, j), align_bytes=64)
+                    nc.sync.dma_start(out=book[:], in_=rows(cb, g)[:, j, :])
+                    if g == 0 and j == 0:
+                        nc.sync.dma_start(offsets[:], offs)
+                    nc.vector.tensor_tensor(part[:, j, :], book[:].indirect(offsets[:]), minus_beta[:], MULT)
+                z = keep.tile([P, 2, T], F32, name="z%d_%d" % (g, h), align_bytes=64)
+                nc.sync.dma_start(out=z[:], in_=rows(zT, g)[:, 2 * h : 2 * h + 2, :])
+                nc.vector.scalar_tensor_tensor(
+                    part[:, 2 * h : 2 * h + 2, :], z[:], BETA, part[:, 2 * h : 2 * h + 2, :], MULT, ADD
+                )
+
+        def add_dy(g, tok, dy):
+            nc.vector.tensor_tensor(packed(g_bf[g][:, tok, :]), planar(parts[g][:, :, tok]), planar(dy), ADD)
+
+        def quantise_g(g, tok):
+            nc.vector.quantize_mx(
+                out=g_codes[:, g, tok].bitcast(E5M2),
+                scales=g_scales[:, g, tok],
+                in_=g_bf[g][:, tok, :].rearrange("p t j -> p (t j)"),
+            )
+
+        def quantise_w(g, cols):
+            nc.vector.quantize_mx(
+                out=w_codes[:, g, cols].bitcast(E4M3),
+                scales=w_scales[:, g, cols],
+                in_=w_bf[:, g, cols, :].rearrange("p d j -> p (d j)"),
+            )
+
+        def multiply(g, m):
+            cols = slice(m * P, (m + 1) * P)
+            nc.tensor.matmul_mx(
+                out=banks[m][:],
+                lhsT=w_codes[:, g, cols].bitcast(E4M3),
+                lhsT_scale=w_scales[:, g, cols],
+                rhs=g_codes[:, g, :].bitcast(E5M2),
+                rhs_scale=g_scales[:, g, :],
+                start=(g == 0),
+                stop=(g == PASSES - 1),
+            )
+
+        def store(m):
+            res = keep.tile([P, T], F32, name="res%d" % m)
+            if m % 2 == 0:
+                nc.scalar.copy(res[:], banks[m][:])
+            else:
+                nc.vector.tensor_copy(res[:], banks[m][:])
+            nc.sync.dma_start(out=out[m * P : (m + 1) * P, :], in_=res[:])
+
+        commitment(0)
+        for h in range(2):
+            dy0 = keep.tile([P, PACK, HALF], F32, name="dy0_%d" % h, align_bytes=64)
+            nc.sync.dma_start(out=dy0[:], in_=rows(dyT, 0)[:, :, halves[h]])
+            add_dy(0, halves[h], dy0[:])
+        commitment(1)
+        quantise_g(0, slice(0, T))
+
+        dy1 = keep.tile([P, PACK, T], F32, name="dy1", align_bytes=64)
+        nc.sync.dma_start(out=dy1[:], in_=rows(dyT, 1))
+        w0 = keep.tile([P, PACK, D], F32, name="w0", align_bytes=64)
+        nc.sync.dma_start(out=w0[:], in_=rows(wm, 0))
+        w1 = []
+        for h in range(2):
+            w1h = keep.tile([P, PACK, 2 * P], F32, name="w1_%d" % h, align_bytes=64)
+            nc.sync.dma_start(out=w1h[:], in_=rows(wm, 1)[:, :, 2 * h * P : 2 * (h + 1) * P])
+            w1.append(w1h)
+
+        for h in range(2):
+            nc.scalar.copy(packed(w_bf[:, 0, halves[h], :]), planar(w0[:, :, halves[h]]))
+        nc.scalar.copy(packed(w_bf[:, 1, halves[0], :]), planar(w1[0][:]))
+        for m in (2, 3):
+            nc.scalar.copy(packed(w_bf[:, 1, m * P : (m + 1) * P, :]), planar(w1[1][:, :, (m - 2) * P : (m - 1) * P]))
+
+        add_dy(1, halves[0], dy1[:, :, halves[0]])
+        add_dy(1, halves[1], dy1[:, :, halves[1]])
+        quantise_w(0, halves[0])
+        multiply(0, 0)
+        multiply(0, 1)
+        quantise_g(1, halves[0])
+        quantise_w(0, halves[1])
+        multiply(0, 2)
+        multiply(0, 3)
+        quantise_g(1, halves[1])
+        quantise_w(1, halves[0])
+        multiply(1, 0)
+        multiply(1, 1)
+        for m in (2, 3):
+            quantise_w(1, slice(m * P, (m + 1) * P))
+            multiply(1, m)
+        for m in range(4):
+            store(m)

@@ -57,20 +57,40 @@ def tile_attend_gvq_s_x_kernel(tc, zT, cb, dyT, wm, offs, out):
         g_bf = [keep.tile([P, T, PACK], BF16, name="g_bf%d" % g, align_bytes=64) for g in range(PASSES)]
         halves = [slice(0, HALF), slice(HALF, T)]
 
-        def commitment(g):
-            part = parts[g]
-            for h in range(2):
-                for j in (2 * h, 2 * h + 1):
-                    book = keep.tile([P, C], F32, name="book%d_%d" % (g, j), align_bytes=64)
-                    nc.sync.dma_start(out=book[:], in_=rows(cb, g)[:, j, :])
-                    if g == 0 and j == 0:
-                        nc.sync.dma_start(offsets[:], offs)
-                    nc.vector.tensor_tensor(part[:, j, :], book[:].indirect(offsets[:]), minus_beta[:], MULT)
-                z = keep.tile([P, 2, T], F32, name="z%d_%d" % (g, h), align_bytes=64)
-                nc.sync.dma_start(out=z[:], in_=rows(zT, g)[:, 2 * h : 2 * h + 2, :])
-                nc.vector.scalar_tensor_tensor(
-                    part[:, 2 * h : 2 * h + 2, :], z[:], BETA, part[:, 2 * h : 2 * h + 2, :], MULT, ADD
-                )
+        def load(name, src):
+            tile = keep.tile(list(src.shape), F32, name=name, align_bytes=64)
+            nc.sync.dma_start(out=tile[:], in_=src)
+            return tile
+
+        def load_book(r):
+            return load("book%d" % r, rows(cb, r // PACK)[:, r % PACK, :])
+
+        def load_z(q):
+            return load("z%d" % q, rows(zT, q // 2)[:, 2 * (q % 2) : 2 * (q % 2) + 2, :])
+
+        books, zs = [load_book(0)], []
+        nc.sync.dma_start(offsets[:], offs)
+        books += [load_book(1), load_book(2)]
+        zs.append(load_z(0))
+        books += [load_book(3), load_book(4)]
+        zs.append(load_z(1))
+        books += [load_book(5), load_book(6)]
+        zs.append(load_z(2))
+        books.append(load_book(7))
+        dy0 = load("dy0", rows(dyT, 0))
+        zs.append(load_z(3))
+        w0 = load("w0", rows(wm, 0))
+        dy1 = [load("dy1_%d" % h, rows(dyT, 1)[:, :, halves[h]]) for h in range(2)]
+        w1 = [load("w1_%d" % h, rows(wm, 1)[:, :, halves[h]]) for h in range(2)]
+
+        def gather(r):
+            nc.vector.tensor_tensor(
+                parts[r // PACK][:, r % PACK, :], books[r][:].indirect(offsets[:]), minus_beta[:], MULT
+            )
+
+        def add_z(q):
+            pair = parts[q // 2][:, 2 * (q % 2) : 2 * (q % 2) + 2, :]
+            nc.vector.scalar_tensor_tensor(pair, zs[q][:], BETA, pair, MULT, ADD)
 
         def add_dy(g, tok, dy):
             nc.vector.tensor_tensor(packed(g_bf[g][:, tok, :]), planar(parts[g][:, :, tok]), planar(dy), ADD)
@@ -109,44 +129,40 @@ def tile_attend_gvq_s_x_kernel(tc, zT, cb, dyT, wm, offs, out):
                 nc.vector.tensor_copy(res[:], banks[m][:])
             nc.sync.dma_start(out=out[m * P : (m + 1) * P, :], in_=res[:])
 
-        commitment(0)
-        for h in range(2):
-            dy0 = keep.tile([P, PACK, HALF], F32, name="dy0_%d" % h, align_bytes=64)
-            nc.sync.dma_start(out=dy0[:], in_=rows(dyT, 0)[:, :, halves[h]])
-            add_dy(0, halves[h], dy0[:])
-        commitment(1)
-        quantise_g(0, slice(0, T))
-
-        dy1 = keep.tile([P, PACK, T], F32, name="dy1", align_bytes=64)
-        nc.sync.dma_start(out=dy1[:], in_=rows(dyT, 1))
-        w0 = keep.tile([P, PACK, D], F32, name="w0", align_bytes=64)
-        nc.sync.dma_start(out=w0[:], in_=rows(wm, 0))
-        w1 = []
-        for h in range(2):
-            w1h = keep.tile([P, PACK, 2 * P], F32, name="w1_%d" % h, align_bytes=64)
-            nc.sync.dma_start(out=w1h[:], in_=rows(wm, 1)[:, :, 2 * h * P : 2 * (h + 1) * P])
-            w1.append(w1h)
-
         for h in range(2):
             nc.scalar.copy(packed(w_bf[:, 0, halves[h], :]), planar(w0[:, :, halves[h]]))
-        nc.scalar.copy(packed(w_bf[:, 1, halves[0], :]), planar(w1[0][:]))
-        for m in (2, 3):
-            nc.scalar.copy(packed(w_bf[:, 1, m * P : (m + 1) * P, :]), planar(w1[1][:, :, (m - 2) * P : (m - 1) * P]))
+        for m in range(4):
+            nc.scalar.copy(
+                packed(w_bf[:, 1, m * P : (m + 1) * P, :]), planar(w1[m // 2][:, :, (m % 2) * P : (m % 2 + 1) * P])
+            )
 
-        add_dy(1, halves[0], dy1[:, :, halves[0]])
-        add_dy(1, halves[1], dy1[:, :, halves[1]])
+        gather(0)
+        gather(1)
+        gather(2)
+        add_z(0)
+        gather(3)
+        gather(4)
+        add_z(1)
+        gather(5)
+        gather(6)
+        add_z(2)
+        gather(7)
+        add_dy(0, slice(0, T), dy0[:])
+        add_z(3)
+        quantise_g(0, slice(0, T))
+        add_dy(1, halves[0], dy1[0][:])
         quantise_w(0, halves[0])
         multiply(0, 0)
         multiply(0, 1)
-        quantise_g(1, halves[0])
+        add_dy(1, halves[1], dy1[1][:])
         quantise_w(0, halves[1])
         multiply(0, 2)
         multiply(0, 3)
+        quantise_g(1, halves[0])
+        quantise_w(1, slice(0, P))
         quantise_g(1, halves[1])
-        quantise_w(1, halves[0])
         multiply(1, 0)
-        multiply(1, 1)
-        for m in (2, 3):
+        for m in (1, 2, 3):
             quantise_w(1, slice(m * P, (m + 1) * P))
             multiply(1, m)
         for m in range(4):

@@ -46,19 +46,19 @@ def tile_attend_gvq_s_x_kernel(tc, zT, cb, dyT, wm, offs, out):
         minus_beta = keep.tile([P, T], F32, name="minus_beta")
         nc.gpsimd.memset(minus_beta[:], -BETA)
 
-        g_codes = keep.tile([P, PASSES, T], U32, name="g_codes", align_bytes=64)
         g_scales = keep.tile([P, PASSES, T], U8, name="g_scales", align_bytes=64)
         w_codes = keep.tile([P, PASSES, D], U32, name="w_codes", align_bytes=64)
         w_scales = keep.tile([P, PASSES, D], U8, name="w_scales", align_bytes=64)
 
-        w_bf = keep.tile([P, PASSES, D, PACK], BF16, name="w_bf", align_bytes=64)
         banks = [psum.tile([P, T], F32, name="bank%d" % m) for m in range(D // P)]
         parts = [keep.tile([P, PACK, T], F32, name="part%d" % g, align_bytes=64) for g in range(PASSES)]
-        g_bf = [keep.tile([P, T, PACK], BF16, name="g_bf%d" % g, align_bytes=64) for g in range(PASSES)]
+        g_rounded = keep.tile([P, T, PACK], BF16, name="g_rounded", align_bytes=64)
+        g_bf = [g_rounded, g_rounded]
+        w_bf = [keep.tile([P, D, PACK], BF16, name="w_bf%d" % g, tag="w_bf%d" % g, align_bytes=64) for g in range(PASSES)]
         halves = [slice(0, HALF), slice(HALF, T)]
 
         def load(name, src):
-            tile = keep.tile(list(src.shape), F32, name=name, align_bytes=64)
+            tile = keep.tile(list(src.shape), F32, name=name, tag=name, align_bytes=64)
             nc.sync.dma_start(out=tile[:], in_=src)
             return tile
 
@@ -80,8 +80,8 @@ def tile_attend_gvq_s_x_kernel(tc, zT, cb, dyT, wm, offs, out):
         dy0 = load("dy0", rows(dyT, 0))
         zs.append(load_z(3))
         w0 = load("w0", rows(wm, 0))
-        dy1 = [load("dy1_%d" % h, rows(dyT, 1)[:, :, halves[h]]) for h in range(2)]
-        w1 = [load("w1_%d" % h, rows(wm, 1)[:, :, halves[h]]) for h in range(2)]
+        dy1 = load("dy1", rows(dyT, 1))
+        w1 = load("w1", rows(wm, 1))
 
         def gather(r):
             nc.vector.tensor_tensor(
@@ -97,44 +97,46 @@ def tile_attend_gvq_s_x_kernel(tc, zT, cb, dyT, wm, offs, out):
 
         def quantise_g(g, tok):
             nc.vector.quantize_mx(
-                out=g_codes[:, g, tok].bitcast(E5M2),
+                out=g_codes[g][:, tok].bitcast(E5M2),
                 scales=g_scales[:, g, tok],
                 in_=g_bf[g][:, tok, :].rearrange("p t j -> p (t j)"),
             )
 
-        def quantise_w(g, cols):
+        def quantise_w(g, span):
             nc.vector.quantize_mx(
-                out=w_codes[:, g, cols].bitcast(E4M3),
-                scales=w_scales[:, g, cols],
-                in_=w_bf[:, g, cols, :].rearrange("p d j -> p (d j)"),
+                out=w_codes[:, g, span].bitcast(E4M3),
+                scales=w_scales[:, g, span],
+                in_=w_bf[g][:, span, :].rearrange("p d j -> p (d j)"),
             )
 
         def multiply(g, m):
-            cols = slice(m * P, (m + 1) * P)
+            span = slice(m * P, (m + 1) * P)
             nc.tensor.matmul_mx(
                 out=banks[m][:],
-                lhsT=w_codes[:, g, cols].bitcast(E4M3),
-                lhsT_scale=w_scales[:, g, cols],
-                rhs=g_codes[:, g, :].bitcast(E5M2),
+                lhsT=w_codes[:, g, span].bitcast(E4M3),
+                lhsT_scale=w_scales[:, g, span],
+                rhs=g_codes[g][:].bitcast(E5M2),
                 rhs_scale=g_scales[:, g, :],
                 start=(g == 0),
                 stop=(g == PASSES - 1),
             )
 
-        def store(m):
-            res = keep.tile([P, T], F32, name="res%d" % m)
-            if m % 2 == 0:
-                nc.scalar.copy(res[:], banks[m][:])
-            else:
-                nc.vector.tensor_copy(res[:], banks[m][:])
-            nc.sync.dma_start(out=out[m * P : (m + 1) * P, :], in_=res[:])
+        def cols(first, last):
+            return slice(first * P, (last + 1) * P)
 
-        for h in range(2):
-            nc.scalar.copy(packed(w_bf[:, 0, halves[h], :]), planar(w0[:, :, halves[h]]))
-        for m in range(4):
-            nc.scalar.copy(
-                packed(w_bf[:, 1, m * P : (m + 1) * P, :]), planar(w1[m // 2][:, :, (m % 2) * P : (m % 2 + 1) * P])
-            )
+        def store(m, tok):
+            res = keep.tile([P, tok.stop - tok.start], F32, name="res%d_%d" % (m, tok.start))
+            if m != 2:
+                nc.scalar.copy(res[:], banks[m][:, tok])
+            else:
+                nc.vector.tensor_copy(res[:], banks[m][:, tok])
+            nc.sync.dma_start(out=out[m * P : (m + 1) * P, tok], in_=res[:])
+
+        def round_w_scalar(g, w, span):
+            nc.scalar.copy(packed(w_bf[g][:, span, :]), planar(w[:, :, span]))
+
+        def round_w_vector(g, w, span):
+            nc.vector.tensor_copy(packed(w_bf[g][:, span, :]), planar(w[:, :, span]))
 
         gather(0)
         gather(1)
@@ -149,21 +151,33 @@ def tile_attend_gvq_s_x_kernel(tc, zT, cb, dyT, wm, offs, out):
         gather(7)
         add_dy(0, slice(0, T), dy0[:])
         add_z(3)
+        round_w_scalar(0, w0, cols(0, 1))
+        round_w_vector(0, w0, cols(2, 3))
+        quantise_w(0, cols(2, 3))
+        quantise_w(0, cols(0, 1))
+        g_codes = [
+            keep.tile([P, T], U32, name="g_codes0", tag="w_bf0", align_bytes=64),
+            keep.tile([P, T], U32, name="g_codes1", align_bytes=64),
+        ]
         quantise_g(0, slice(0, T))
-        add_dy(1, halves[0], dy1[0][:])
-        quantise_w(0, halves[0])
-        multiply(0, 0)
-        multiply(0, 1)
-        add_dy(1, halves[1], dy1[1][:])
-        quantise_w(0, halves[1])
-        multiply(0, 2)
-        multiply(0, 3)
-        quantise_g(1, halves[0])
-        quantise_w(1, slice(0, P))
-        quantise_g(1, halves[1])
-        multiply(1, 0)
-        for m in (1, 2, 3):
-            quantise_w(1, slice(m * P, (m + 1) * P))
-            multiply(1, m)
         for m in range(4):
-            store(m)
+            multiply(0, m)
+        add_dy(1, halves[0], dy1[:, :, halves[0]])
+        add_dy(1, halves[1], dy1[:, :, halves[1]])
+        quantise_g(1, halves[0])
+        round_w_scalar(1, w1, cols(0, 0))
+        round_w_scalar(1, w1, cols(1, 1))
+        quantise_g(1, halves[1])
+        quantise_w(1, cols(0, 0))
+        multiply(1, 0)
+        round_w_vector(1, w1, cols(2, 2))
+        quantise_w(1, cols(1, 1))
+        multiply(1, 1)
+        round_w_vector(1, w1, cols(3, 3))
+        for m in (2, 3):
+            quantise_w(1, cols(m, m))
+            multiply(1, m)
+        store(0, halves[0])
+        store(0, halves[1])
+        for m in (1, 2, 3):
+            store(m, slice(0, T))

@@ -15,6 +15,8 @@ E4M3 = mybir.dt.float8_e4m3fn_x4
 E5M2 = mybir.dt.float8_e5m2_x4
 MULT = mybir.AluOpType.mult
 ADD = mybir.AluOpType.add
+SUB = mybir.AluOpType.subtract
+COPY = mybir.ActivationFunctionType.Copy
 
 P = 128
 PACK = 4
@@ -43,19 +45,16 @@ def tile_attend_gvq_s_x_kernel(tc, zT, cb, dyT, wm, offs, out):
         psum = ctx.enter_context(tc.psum_pool(name="psum", bufs=1))
 
         offsets = keep.tile([P, T // 16], U16, name="offsets")
-        minus_beta = keep.tile([P, T], F32, name="minus_beta")
-        nc.gpsimd.memset(minus_beta[:], -BETA)
-
-        g_scales = keep.tile([P, PASSES, T], U8, name="g_scales", align_bytes=64)
+        g_codes = {1: keep.tile([P, T], U32, name="g_codes1", align_bytes=64)}
+        g_scales = [keep.tile([P, T], U8, name="g_scales%d" % g, align_bytes=64) for g in range(PASSES)]
         w_codes = keep.tile([P, PASSES, D], U32, name="w_codes", align_bytes=64)
         w_scales = keep.tile([P, PASSES, D], U8, name="w_scales", align_bytes=64)
-
         banks = [psum.tile([P, T], F32, name="bank%d" % m) for m in range(D // P)]
         parts = [keep.tile([P, PACK, T], F32, name="part%d" % g, align_bytes=64) for g in range(PASSES)]
-        g_rounded = keep.tile([P, T, PACK], BF16, name="g_rounded", align_bytes=64)
-        g_bf = [g_rounded, g_rounded]
-        w_bf = [keep.tile([P, D, PACK], BF16, name="w_bf%d" % g, tag="w_bf%d" % g, align_bytes=64) for g in range(PASSES)]
+        g_bf = [keep.tile([P, T, PACK], BF16, name="g_bf%d" % g, align_bytes=64) for g in range(PASSES)]
+        w_bf = [keep.tile([P, D, PACK], BF16, name="w_bf%d" % g, align_bytes=64) for g in range(PASSES)]
         halves = [slice(0, HALF), slice(HALF, T)]
+        every = slice(0, T)
 
         def load(name, src):
             tile = keep.tile(list(src.shape), F32, name=name, tag=name, align_bytes=64)
@@ -65,40 +64,16 @@ def tile_attend_gvq_s_x_kernel(tc, zT, cb, dyT, wm, offs, out):
         def load_book(r):
             return load("book%d" % r, rows(cb, r // PACK)[:, r % PACK, :])
 
-        def load_z(q):
-            return load("z%d" % q, rows(zT, q // 2)[:, 2 * (q % 2) : 2 * (q % 2) + 2, :])
+        def load_pair(name, x, q):
+            return load("%s%d" % (name, q), rows(x, q // 2)[:, 2 * (q % 2) : 2 * (q % 2) + 2, :])
 
-        books, zs = [load_book(0)], []
-        nc.sync.dma_start(offsets[:], offs)
-        books += [load_book(1), load_book(2)]
-        zs.append(load_z(0))
-        books += [load_book(3), load_book(4)]
-        zs.append(load_z(1))
-        books += [load_book(5), load_book(6)]
-        zs.append(load_z(2))
-        books.append(load_book(7))
-        dy0 = load("dy0", rows(dyT, 0))
-        zs.append(load_z(3))
-        w0 = load("w0", rows(wm, 0))
-        dy1 = load("dy1", rows(dyT, 1))
-        w1 = load("w1", rows(wm, 1))
-
-        def gather(r):
-            nc.vector.tensor_tensor(
-                parts[r // PACK][:, r % PACK, :], books[r][:].indirect(offsets[:]), minus_beta[:], MULT
-            )
-
-        def add_z(q):
-            pair = parts[q // 2][:, 2 * (q % 2) : 2 * (q % 2) + 2, :]
-            nc.vector.scalar_tensor_tensor(pair, zs[q][:], BETA, pair, MULT, ADD)
-
-        def add_dy(g, tok, dy):
-            nc.vector.tensor_tensor(packed(g_bf[g][:, tok, :]), planar(parts[g][:, :, tok]), planar(dy), ADD)
+        def cols(first, last):
+            return slice(first * P, (last + 1) * P)
 
         def quantise_g(g, tok):
             nc.vector.quantize_mx(
                 out=g_codes[g][:, tok].bitcast(E5M2),
-                scales=g_scales[:, g, tok],
+                scales=g_scales[g][:, tok],
                 in_=g_bf[g][:, tok, :].rearrange("p t j -> p (t j)"),
             )
 
@@ -116,68 +91,91 @@ def tile_attend_gvq_s_x_kernel(tc, zT, cb, dyT, wm, offs, out):
                 lhsT=w_codes[:, g, span].bitcast(E4M3),
                 lhsT_scale=w_scales[:, g, span],
                 rhs=g_codes[g][:].bitcast(E5M2),
-                rhs_scale=g_scales[:, g, :],
+                rhs_scale=g_scales[g][:],
                 start=(g == 0),
                 stop=(g == PASSES - 1),
             )
 
-        def cols(first, last):
-            return slice(first * P, (last + 1) * P)
-
-        def store(m, tok):
+        def store(m, tok, engine):
             res = keep.tile([P, tok.stop - tok.start], F32, name="res%d_%d" % (m, tok.start))
-            if m != 2:
+            if engine == "scalar":
                 nc.scalar.copy(res[:], banks[m][:, tok])
             else:
                 nc.vector.tensor_copy(res[:], banks[m][:, tok])
             nc.sync.dma_start(out=out[m * P : (m + 1) * P, tok], in_=res[:])
 
-        def round_w_scalar(g, w, span):
-            nc.scalar.copy(packed(w_bf[g][:, span, :]), planar(w[:, :, span]))
+        def round_w_scalar(g, span, w):
+            nc.scalar.copy(packed(w_bf[g][:, span, :]), planar(w))
 
-        def round_w_vector(g, w, span):
-            nc.vector.tensor_copy(packed(w_bf[g][:, span, :]), planar(w[:, :, span]))
+        def round_w_vector(g, span, w):
+            nc.vector.tensor_copy(packed(w_bf[g][:, span, :]), planar(w))
 
-        gather(0)
-        gather(1)
-        gather(2)
-        add_z(0)
-        gather(3)
-        gather(4)
-        add_z(1)
-        gather(5)
-        gather(6)
-        add_z(2)
-        gather(7)
-        add_dy(0, slice(0, T), dy0[:])
-        add_z(3)
-        round_w_scalar(0, w0, cols(0, 1))
-        round_w_vector(0, w0, cols(2, 3))
-        quantise_w(0, cols(2, 3))
-        quantise_w(0, cols(0, 1))
-        g_codes = [
-            keep.tile([P, T], U32, name="g_codes0", tag="w_bf0", align_bytes=64),
-            keep.tile([P, T], U32, name="g_codes1", align_bytes=64),
-        ]
-        quantise_g(0, slice(0, T))
-        for m in range(4):
-            multiply(0, m)
-        add_dy(1, halves[0], dy1[:, :, halves[0]])
-        add_dy(1, halves[1], dy1[:, :, halves[1]])
+        def load_planes(name, x, r, n):
+            return load("%s%d" % (name, r), rows(x, r // PACK)[:, r % PACK : r % PACK + n, :])
+
+        def gather(r):
+            nc.vector.tensor_tensor(
+                parts[r // PACK][:, r % PACK, :], books[r][:].indirect(offsets[:]), zs[r // 2][:, r % 2, :], SUB
+            )
+
+        def scale(r, n):
+            planes = parts[r // PACK][:, r % PACK : r % PACK + n, :]
+            nc.scalar.activation(planes, planes, COPY, scale=-BETA)
+
+        def add_dy(g, tok):
+            nc.vector.tensor_tensor(
+                packed(g_bf[g][:, tok, :]), planar(parts[g][:, :, tok]), planar(dys[g][:, :, tok]), ADD
+            )
+
+        def round_w(g, first, last, how):
+            how(g, cols(first, last), ws[g][:, :, cols(first, last)])
+
+        def block(g, first, last):
+            quantise_w(g, cols(first, last))
+            for m in range(first, last + 1):
+                multiply(g, m)
+
+        books, zs, dys, ws = {}, {}, {}, {}
+        for kind, r in [("z", 0), ("book", 0), ("book", 1), ("z", 1), ("book", 2), ("book", 3), ("dy", 0), ("z", 2), ("book", 4), ("book", 5), ("z", 3), ("book", 6), ("book", 7), ("dy", 1), ("w", 0), ("w", 1)]:
+            if kind == "z":
+                zs[r] = load_planes("z", zT, 2 * r, 2)
+            elif kind == "dy":
+                dys[r] = load("dy%d" % r, rows(dyT, r))
+            elif kind == "book":
+                books[r] = load_book(r)
+                if r == 0:
+                    nc.sync.dma_start(offsets[:], offs)
+            else:
+                ws[r] = load("w%d" % r, rows(wm, r))
+
+        for r in range(4):
+            gather(r)
+            scale(r, 1)
+        add_dy(0, every)
+        for r in range(4, 8):
+            gather(r)
+            scale(r, 1)
+        g_codes[0] = keep.tile([P, T], U32, name="g_codes0", tag="book7", align_bytes=64)
+        quantise_g(0, every)
+        add_dy(1, halves[0])
+        add_dy(1, halves[1])
         quantise_g(1, halves[0])
-        round_w_scalar(1, w1, cols(0, 0))
-        round_w_scalar(1, w1, cols(1, 1))
         quantise_g(1, halves[1])
-        quantise_w(1, cols(0, 0))
-        multiply(1, 0)
-        round_w_vector(1, w1, cols(2, 2))
-        quantise_w(1, cols(1, 1))
-        multiply(1, 1)
-        round_w_vector(1, w1, cols(3, 3))
-        for m in (2, 3):
-            quantise_w(1, cols(m, m))
-            multiply(1, m)
-        store(0, halves[0])
-        store(0, halves[1])
-        for m in (1, 2, 3):
-            store(m, slice(0, T))
+        for m in range(4):
+            round_w(0, m, m, round_w_scalar)
+        for m in range(3):
+            block(0, m, m)
+        round_w(1, 0, 0, round_w_vector)
+        round_w(1, 1, 1, round_w_vector)
+        round_w(1, 2, 2, round_w_scalar)
+        round_w(1, 3, 3, round_w_scalar)
+        block(1, 0, 0)
+        block(1, 1, 1)
+        block(0, 3, 3)
+        block(1, 2, 2)
+        block(1, 3, 3)
+        store(0, halves[0], "scalar")
+        store(0, halves[1], "scalar")
+        store(1, every, "vector")
+        store(2, every, "scalar")
+        store(3, every, "vector")

@@ -114,68 +114,98 @@ def tile_attend_gvq_s_x_kernel(tc, zT, cb, dyT, wm, offs, out):
             return load("%s%d" % (name, r), rows(x, r // PACK)[:, r % PACK : r % PACK + n, :])
 
         def gather(r):
+            z, first = zs[r]
             nc.vector.tensor_tensor(
-                parts[r // PACK][:, r % PACK, :], books[r][:].indirect(offsets[:]), zs[r // 2][:, r % 2, :], SUB
+                parts[r // PACK][:, r % PACK, :], books[r][:].indirect(offsets[:]), z[:, r - first, :], SUB
             )
 
-        def scale(r, n):
-            planes = parts[r // PACK][:, r % PACK : r % PACK + n, :]
+        def scale(r, n, tok=every):
+            planes = parts[r // PACK][:, r % PACK : r % PACK + n, tok]
             nc.scalar.activation(planes, planes, COPY, scale=-BETA)
 
-        def add_dy(g, tok):
-            nc.vector.tensor_tensor(
-                packed(g_bf[g][:, tok, :]), planar(parts[g][:, :, tok]), planar(dys[g][:, :, tok]), ADD
-            )
+        def add_dy(g, tok, dy):
+            nc.vector.tensor_tensor(packed(g_bf[g][:, tok, :]), planar(parts[g][:, :, tok]), planar(dy), ADD)
+
+        def join_dy(g, tok, dy):
+            nc.vector.scalar_tensor_tensor(parts[g][:, :, tok], parts[g][:, :, tok], -BETA, dy, MULT, ADD)
+
+        def round_g(g, tok):
+            nc.scalar.copy(packed(g_bf[g][:, tok, :]), planar(parts[g][:, :, tok]))
 
         def round_w(g, first, last, how):
-            how(g, cols(first, last), ws[g][:, :, cols(first, last)])
+            tile, base = ws[g, first]
+            how(g, cols(first, last), tile[:, :, cols(first - base, last - base)])
 
         def block(g, first, last):
             quantise_w(g, cols(first, last))
             for m in range(first, last + 1):
                 multiply(g, m)
 
-        books, zs, dys, ws = {}, {}, {}, {}
-        for kind, r in [("z", 0), ("book", 0), ("book", 1), ("z", 1), ("book", 2), ("book", 3), ("dy", 0), ("z", 2), ("book", 4), ("book", 5), ("z", 3), ("book", 6), ("book", 7), ("dy", 1), ("w", 0), ("w", 1)]:
-            if kind == "z":
-                zs[r] = load_planes("z", zT, 2 * r, 2)
-            elif kind == "dy":
-                dys[r] = load("dy%d" % r, rows(dyT, r))
-            elif kind == "book":
-                books[r] = load_book(r)
-                if r == 0:
-                    nc.sync.dma_start(offsets[:], offs)
-            else:
-                ws[r] = load("w%d" % r, rows(wm, r))
+        def load_w(g, first, last):
+            tile = load("w%d_%d" % (g, first), rows(wm, g)[:, :, cols(first, last)])
+            for m in range(first, last + 1):
+                ws[g, m] = (tile, first)
+
+        books, zs, ws = {}, {}, {}
+
+        def load_z(r, n):
+            tile = load_planes("z", zT, r, n)
+            for i in range(n):
+                zs[r + i] = (tile, r)
+
+        def load_book_pair(r):
+            src = rows(cb, r // PACK)[:, r % PACK : r % PACK + 2, :].rearrange("p j c -> p (j c)")
+            books[r] = load("book%d" % r, src)
+
+        def move_book(r):
+            books[r] = keep.tile([P, C], F32, name="book%d" % r, tag="book%d" % r, align_bytes=64)
+            nc.scalar.activation(books[r][:], books[r - 1][:, C:], COPY)
+
+        for q in range(4):
+            load_z(2 * q, 2)
+            books[2 * q] = load_book(2 * q)
+            if q == 0:
+                nc.sync.dma_start(offsets[:], offs)
+            books[2 * q + 1] = load_book(2 * q + 1)
+            if q == 1:
+                dy0 = load("dy0", rows(dyT, 0))
+        dy1 = load("dy1", rows(dyT, 1))
+        load_w(0, 0, 3)
+        load_w(1, 0, 1)
+        load_w(1, 2, 3)
 
         for r in range(4):
             gather(r)
             scale(r, 1)
-        add_dy(0, every)
+        add_dy(0, every, dy0[:])
         for r in range(4, 8):
             gather(r)
             scale(r, 1)
         g_codes[0] = keep.tile([P, T], U32, name="g_codes0", tag="book7", align_bytes=64)
         quantise_g(0, every)
-        add_dy(1, halves[0])
-        add_dy(1, halves[1])
+        add_dy(1, halves[0], dy1[:, :, halves[0]])
+        add_dy(1, halves[1], dy1[:, :, halves[1]])
         quantise_g(1, halves[0])
         quantise_g(1, halves[1])
-        for m in range(4):
-            round_w(0, m, m, round_w_scalar)
-        for m in range(3):
-            block(0, m, m)
+        round_w(0, 0, 0, round_w_scalar)
+        round_w(0, 1, 1, round_w_scalar)
+        round_w(0, 2, 2, round_w_scalar)
+        round_w(1, 1, 1, round_w_scalar)
+        round_w(0, 3, 3, round_w_scalar)
+        block(0, 0, 0)
         round_w(1, 0, 0, round_w_vector)
-        round_w(1, 1, 1, round_w_vector)
-        round_w(1, 2, 2, round_w_scalar)
-        round_w(1, 3, 3, round_w_scalar)
+        block(0, 1, 1)
         block(1, 0, 0)
         block(1, 1, 1)
+        block(0, 2, 2)
+        round_w(1, 2, 2, round_w_vector)
         block(0, 3, 3)
+        round_w(1, 3, 3, round_w_vector)
         block(1, 2, 2)
         block(1, 3, 3)
         store(0, halves[0], "scalar")
         store(0, halves[1], "scalar")
-        store(1, every, "vector")
-        store(2, every, "scalar")
-        store(3, every, "vector")
+        store(1, every, "scalar")
+        store(2, every, "vector")
+        store(3, halves[0], "scalar")
+        store(3, halves[1], "scalar")

@@ -161,23 +161,25 @@ def tile_attend_gvq_s_x_kernel(tc, zT, cb, dyT, wm, offs, out):
             books[r] = keep.tile([P, C], F32, name="book%d" % r, tag="book%d" % r, align_bytes=64)
             nc.scalar.activation(books[r][:], books[r - 1][:, C:], COPY)
 
-        for q in range(4):
-            load_z(2 * q, 2)
-            books[2 * q] = load_book(2 * q)
-            if q == 0:
-                nc.sync.dma_start(offsets[:], offs)
-            books[2 * q + 1] = load_book(2 * q + 1)
-            if q == 1:
-                dy0 = load("dy0", rows(dyT, 0))
+        load_book_pair(0)
+        nc.sync.dma_start(offsets[:], offs)
+        load_z(0, 4)
+        load_book_pair(2)
+        dy0 = load("dy0", rows(dyT, 0))
+        load_z(4, 4)
+        for r in range(4, 8):
+            books[r] = load_book(r)
         dy1 = load("dy1", rows(dyT, 1))
         load_w(0, 0, 3)
         load_w(1, 0, 1)
         load_w(1, 2, 3)
 
+        move_book(1)
+        move_book(3)
         for r in range(4):
             gather(r)
-            scale(r, 1)
-        add_dy(0, every, dy0[:])
+        join_dy(0, every, dy0[:])
+        round_g(0, every)
         for r in range(4, 8):
             gather(r)
             scale(r, 1)

@@ -55,20 +55,56 @@ def tile_attend_gvq_s_x_kernel(tc, zT, cb, dyT, wm, offs, out):
         w_bf = [keep.tile([P, D, PACK], BF16, name="w_bf%d" % g, align_bytes=64) for g in range(PASSES)]
         halves = [slice(0, HALF), slice(HALF, T)]
         every = slice(0, T)
+        books, dys, zs, ws = {}, {}, {}, {}
+
+        def clock(name, ap):
+            t = keep.tile([P, 1], ap.dtype, name=name)
+            nc.gpsimd.tensor_copy(t[:], ap)
 
         def load(name, src):
             tile = keep.tile(list(src.shape), F32, name=name, tag=name, align_bytes=64)
             nc.sync.dma_start(out=tile[:], in_=src)
             return tile
 
-        def load_book(r):
-            return load("book%d" % r, rows(cb, r // PACK)[:, r % PACK, :])
-
-        def load_pair(name, x, q):
-            return load("%s%d" % (name, q), rows(x, q // 2)[:, 2 * (q % 2) : 2 * (q % 2) + 2, :])
-
         def cols(first, last):
             return slice(first * P, (last + 1) * P)
+
+        def load_book(r, n):
+            src = rows(cb, r // PACK)[:, r % PACK : r % PACK + n, :].rearrange("p j c -> p (j c)")
+            books[r] = load("book%d" % r, src)
+
+        def move_book(r, source):
+            books[r] = keep.tile([P, C], F32, name="book%d" % r, tag="book%d" % r, align_bytes=64)
+            nc.scalar.activation(books[r][:], books[source][:, (r - source) * C : (r - source + 1) * C], COPY)
+
+        def load_dy(r, n):
+            tile = load("dy%d" % r, rows(dyT, r // PACK)[:, r % PACK : r % PACK + n, :])
+            for i in range(n):
+                dys[r + i] = (tile, r)
+
+        def load_z(g):
+            zs[g] = load("z%d" % g, rows(zT, g))
+
+        def load_w(g, first, last):
+            tile = load("w%d_%d" % (g, first), rows(wm, g)[:, :, cols(first, last)])
+            for m in range(first, last + 1):
+                ws[g, m] = (tile, first)
+
+        def scale_dy(r, n):
+            dy, first = dys[r]
+            planes = dy[:, r - first : r - first + n, :]
+            nc.scalar.activation(planes, planes, COPY, scale=1.0 / BETA)
+
+        def gather(r):
+            dy, first = dys[r]
+            nc.vector.tensor_tensor(
+                parts[r // PACK][:, r % PACK, :], books[r][:].indirect(offsets[:]), dy[:, r - first, :], SUB
+            )
+
+        def join_z(g, tok):
+            nc.vector.tensor_tensor(
+                packed(g_bf[g][:, tok, :]), planar(zs[g][:, :, tok]), planar(parts[g][:, :, tok]), SUB
+            )
 
         def quantise_g(g, tok):
             nc.vector.quantize_mx(
@@ -77,7 +113,17 @@ def tile_attend_gvq_s_x_kernel(tc, zT, cb, dyT, wm, offs, out):
                 in_=g_bf[g][:, tok, :].rearrange("p t j -> p (t j)"),
             )
 
-        def quantise_w(g, span):
+        def round_w(g, first, last, engine):
+            tile, base = ws[g, first]
+            src = planar(tile[:, :, cols(first - base, last - base)])
+            dst = packed(w_bf[g][:, cols(first, last), :])
+            if engine == "scalar":
+                nc.scalar.copy(dst, src)
+            else:
+                nc.vector.tensor_copy(dst, src)
+
+        def quantise_w(g, first, last):
+            span = cols(first, last)
             nc.vector.quantize_mx(
                 out=w_codes[:, g, span].bitcast(E4M3),
                 scales=w_scales[:, g, span],
@@ -85,7 +131,7 @@ def tile_attend_gvq_s_x_kernel(tc, zT, cb, dyT, wm, offs, out):
             )
 
         def multiply(g, m):
-            span = slice(m * P, (m + 1) * P)
+            span = cols(m, m)
             nc.tensor.matmul_mx(
                 out=banks[m][:],
                 lhsT=w_codes[:, g, span].bitcast(E4M3),
@@ -96,113 +142,62 @@ def tile_attend_gvq_s_x_kernel(tc, zT, cb, dyT, wm, offs, out):
                 stop=(g == PASSES - 1),
             )
 
-        def store(m, tok, engine):
-            res = keep.tile([P, tok.stop - tok.start], F32, name="res%d_%d" % (m, tok.start))
-            if engine == "scalar":
-                nc.scalar.copy(res[:], banks[m][:, tok])
-            else:
-                nc.vector.tensor_copy(res[:], banks[m][:, tok])
-            nc.sync.dma_start(out=out[m * P : (m + 1) * P, tok], in_=res[:])
-
-        def round_w_scalar(g, span, w):
-            nc.scalar.copy(packed(w_bf[g][:, span, :]), planar(w))
-
-        def round_w_vector(g, span, w):
-            nc.vector.tensor_copy(packed(w_bf[g][:, span, :]), planar(w))
-
-        def load_planes(name, x, r, n):
-            return load("%s%d" % (name, r), rows(x, r // PACK)[:, r % PACK : r % PACK + n, :])
-
-        def gather(r):
-            z, first = zs[r]
-            nc.vector.tensor_tensor(
-                parts[r // PACK][:, r % PACK, :], books[r][:].indirect(offsets[:]), z[:, r - first, :], SUB
-            )
-
-        def scale(r, n, tok=every):
-            planes = parts[r // PACK][:, r % PACK : r % PACK + n, tok]
-            nc.scalar.activation(planes, planes, COPY, scale=-BETA)
-
-        def add_dy(g, tok, dy):
-            nc.vector.tensor_tensor(packed(g_bf[g][:, tok, :]), planar(parts[g][:, :, tok]), planar(dy), ADD)
-
-        def join_dy(g, tok, dy):
-            nc.vector.scalar_tensor_tensor(parts[g][:, :, tok], parts[g][:, :, tok], -BETA, dy, MULT, ADD)
-
-        def round_g(g, tok):
-            nc.scalar.copy(packed(g_bf[g][:, tok, :]), planar(parts[g][:, :, tok]))
-
-        def round_w(g, first, last, how):
-            tile, base = ws[g, first]
-            how(g, cols(first, last), tile[:, :, cols(first - base, last - base)])
-
         def block(g, first, last):
-            quantise_w(g, cols(first, last))
+            quantise_w(g, first, last)
             for m in range(first, last + 1):
                 multiply(g, m)
 
-        def load_w(g, first, last):
-            tile = load("w%d_%d" % (g, first), rows(wm, g)[:, :, cols(first, last)])
-            for m in range(first, last + 1):
-                ws[g, m] = (tile, first)
+        def store(m, tok, engine):
+            res = keep.tile([P, tok.stop - tok.start], F32, name="res%d_%d" % (m, tok.start))
+            if engine == "scalar":
+                nc.scalar.activation(res[:], banks[m][:, tok], COPY, scale=BETA)
+            else:
+                nc.vector.tensor_scalar_mul(res[:], banks[m][:, tok], BETA)
+            nc.sync.dma_start(out=out[m * P : (m + 1) * P, tok], in_=res[:])
 
-        books, zs, ws = {}, {}, {}
-
-        def load_z(r, n):
-            tile = load_planes("z", zT, r, n)
-            for i in range(n):
-                zs[r + i] = (tile, r)
-
-        def load_book_pair(r):
-            src = rows(cb, r // PACK)[:, r % PACK : r % PACK + 2, :].rearrange("p j c -> p (j c)")
-            books[r] = load("book%d" % r, src)
-
-        def move_book(r):
-            books[r] = keep.tile([P, C], F32, name="book%d" % r, tag="book%d" % r, align_bytes=64)
-            nc.scalar.activation(books[r][:], books[r - 1][:, C:], COPY)
-
-        load_book_pair(0)
+        load_dy(0, 4)
         nc.sync.dma_start(offsets[:], offs)
-        load_z(0, 4)
-        load_book_pair(2)
-        dy0 = load("dy0", rows(dyT, 0))
-        load_z(4, 4)
+        load_book(0, 2)
+        load_book(2, 2)
+        load_z(0)
+        load_dy(4, 4)
         for r in range(4, 8):
-            books[r] = load_book(r)
-        dy1 = load("dy1", rows(dyT, 1))
+            load_book(r, 1)
+        load_z(1)
         load_w(0, 0, 3)
         load_w(1, 0, 1)
         load_w(1, 2, 3)
 
-        move_book(1)
-        move_book(3)
+        scale_dy(0, 2)
+        scale_dy(2, 2)
+        move_book(1, 0)
+        move_book(3, 2)
         for r in range(4):
             gather(r)
-        join_dy(0, every, dy0[:])
-        round_g(0, every)
+        join_z(0, every)
         for r in range(4, 8):
+            scale_dy(r, 1)
             gather(r)
-            scale(r, 1)
         g_codes[0] = keep.tile([P, T], U32, name="g_codes0", tag="book7", align_bytes=64)
         quantise_g(0, every)
-        add_dy(1, halves[0], dy1[:, :, halves[0]])
-        add_dy(1, halves[1], dy1[:, :, halves[1]])
+        join_z(1, halves[0])
+        join_z(1, halves[1])
         quantise_g(1, halves[0])
         quantise_g(1, halves[1])
-        round_w(0, 0, 0, round_w_scalar)
-        round_w(0, 1, 1, round_w_scalar)
-        round_w(0, 2, 2, round_w_scalar)
-        round_w(1, 1, 1, round_w_scalar)
-        round_w(0, 3, 3, round_w_scalar)
+        round_w(0, 0, 0, "scalar")
+        round_w(0, 1, 1, "scalar")
+        round_w(0, 2, 2, "scalar")
+        round_w(1, 1, 1, "scalar")
+        round_w(0, 3, 3, "scalar")
         block(0, 0, 0)
-        round_w(1, 0, 0, round_w_vector)
+        round_w(1, 0, 0, "vector")
         block(0, 1, 1)
         block(1, 0, 0)
         block(1, 1, 1)
         block(0, 2, 2)
-        round_w(1, 2, 2, round_w_vector)
+        round_w(1, 2, 2, "vector")
         block(0, 3, 3)
-        round_w(1, 3, 3, round_w_vector)
+        round_w(1, 3, 3, "vector")
         block(1, 2, 2)
         block(1, 3, 3)
         store(0, halves[0], "scalar")

@@ -47,15 +47,13 @@ def tile_attend_gvq_s_x_kernel(tc, zT, cb, dyT, wm, offs, out):
         offsets = keep.tile([P, T // 16], U16, name="offsets")
         g_codes = {1: keep.tile([P, T], U32, name="g_codes1", align_bytes=64)}
         g_scales = [keep.tile([P, T], U8, name="g_scales%d" % g, align_bytes=64) for g in range(PASSES)]
-        w_codes = keep.tile([P, PASSES, D], U32, name="w_codes", align_bytes=64)
         w_scales = keep.tile([P, PASSES, D], U8, name="w_scales", align_bytes=64)
         banks = [psum.tile([P, T], F32, name="bank%d" % m) for m in range(D // P)]
         parts = [keep.tile([P, PACK, T], F32, name="part%d" % g, align_bytes=64) for g in range(PASSES)]
         g_bf = [keep.tile([P, T, PACK], BF16, name="g_bf%d" % g, align_bytes=64) for g in range(PASSES)]
-        w_bf = [keep.tile([P, D, PACK], BF16, name="w_bf%d" % g, align_bytes=64) for g in range(PASSES)]
         halves = [slice(0, HALF), slice(HALF, T)]
         every = slice(0, T)
-        books, dys, zs, ws = {}, {}, {}, {}
+        books, dys, zs, ws, w_bf, w_codes = {}, {}, {}, {}, {}, {}
 
         def clock(name, ap):
             t = keep.tile([P, 1], ap.dtype, name=name)
@@ -113,28 +111,39 @@ def tile_attend_gvq_s_x_kernel(tc, zT, cb, dyT, wm, offs, out):
                 in_=g_bf[g][:, tok, :].rearrange("p t j -> p (t j)"),
             )
 
+        def rounded_tile(g, first, last):
+            name = "w_bf%d_%d" % (g, first)
+            tile = keep.tile([P, (last - first + 1) * P, PACK], BF16, name=name, tag=name, align_bytes=64)
+            for m in range(first, last + 1):
+                w_bf[g, m] = (tile, first)
+
         def round_w(g, first, last, engine):
             tile, base = ws[g, first]
             src = planar(tile[:, :, cols(first - base, last - base)])
-            dst = packed(w_bf[g][:, cols(first, last), :])
+            tile, base = w_bf[g, first]
+            dst = packed(tile[:, cols(first - base, last - base), :])
             if engine == "scalar":
                 nc.scalar.copy(dst, src)
             else:
                 nc.vector.tensor_copy(dst, src)
 
-        def quantise_w(g, first, last):
-            span = cols(first, last)
+        def quantise_w(g, first, last, tag):
+            name = "w_codes%d_%d" % (g, first)
+            codes = keep.tile([P, (last - first + 1) * P], U32, name=name, tag=tag or name, align_bytes=64)
+            for m in range(first, last + 1):
+                w_codes[g, m] = codes[:, cols(m - first, m - first)]
+            tile, base = w_bf[g, first]
             nc.vector.quantize_mx(
-                out=w_codes[:, g, span].bitcast(E4M3),
-                scales=w_scales[:, g, span],
-                in_=w_bf[g][:, span, :].rearrange("p d j -> p (d j)"),
+                out=codes[:].bitcast(E4M3),
+                scales=w_scales[:, g, cols(first, last)],
+                in_=tile[:, cols(first - base, last - base), :].rearrange("p d j -> p (d j)"),
             )
 
         def multiply(g, m):
             span = cols(m, m)
             nc.tensor.matmul_mx(
                 out=banks[m][:],
-                lhsT=w_codes[:, g, span].bitcast(E4M3),
+                lhsT=w_codes[g, m].bitcast(E4M3),
                 lhsT_scale=w_scales[:, g, span],
                 rhs=g_codes[g][:].bitcast(E5M2),
                 rhs_scale=g_scales[g][:],
@@ -142,8 +151,8 @@ def tile_attend_gvq_s_x_kernel(tc, zT, cb, dyT, wm, offs, out):
                 stop=(g == PASSES - 1),
             )
 
-        def block(g, first, last):
-            quantise_w(g, first, last)
+        def block(g, first, last, tag=None):
+            quantise_w(g, first, last, tag)
             for m in range(first, last + 1):
                 multiply(g, m)
 
@@ -155,9 +164,10 @@ def tile_attend_gvq_s_x_kernel(tc, zT, cb, dyT, wm, offs, out):
                 nc.vector.tensor_scalar_mul(res[:], banks[m][:, tok], BETA)
             nc.sync.dma_start(out=out[m * P : (m + 1) * P, tok], in_=res[:])
 
-        load_dy(0, 4)
+        load_dy(0, 2)
         nc.sync.dma_start(offsets[:], offs)
         load_book(0, 2)
+        load_dy(2, 2)
         load_book(2, 2)
         load_z(0)
         load_dy(4, 4)
@@ -169,40 +179,40 @@ def tile_attend_gvq_s_x_kernel(tc, zT, cb, dyT, wm, offs, out):
         load_w(1, 2, 3)
 
         scale_dy(0, 2)
-        scale_dy(2, 2)
         move_book(1, 0)
+        scale_dy(2, 2)
         move_book(3, 2)
         for r in range(4):
             gather(r)
         join_z(0, every)
+        g_codes[0] = keep.tile([P, T], U32, name="g_codes0", align_bytes=64)
+        quantise_g(0, every)
         for r in range(4, 8):
             scale_dy(r, 1)
             gather(r)
-        g_codes[0] = keep.tile([P, T], U32, name="g_codes0", tag="book7", align_bytes=64)
-        quantise_g(0, every)
         join_z(1, halves[0])
         join_z(1, halves[1])
         quantise_g(1, halves[0])
         quantise_g(1, halves[1])
-        round_w(0, 0, 0, "scalar")
-        round_w(0, 1, 1, "scalar")
-        round_w(0, 2, 2, "scalar")
-        round_w(1, 1, 1, "scalar")
-        round_w(0, 3, 3, "scalar")
+        rounded_tile(0, 0, 3)
+        for m in range(4):
+            rounded_tile(1, m, m)
+            round_w(0, m, m, "scalar")
         block(0, 0, 0)
-        round_w(1, 0, 0, "vector")
         block(0, 1, 1)
+        round_w(1, 0, 0, "vector")
+        round_w(1, 1, 1, "vector")
         block(1, 0, 0)
         block(1, 1, 1)
-        block(0, 2, 2)
+        block(0, 2, 3, "w_bf1_0")
         round_w(1, 2, 2, "vector")
-        block(0, 3, 3)
         round_w(1, 3, 3, "vector")
         block(1, 2, 2)
         block(1, 3, 3)
         store(0, halves[0], "scalar")
         store(0, halves[1], "scalar")
         store(1, every, "scalar")
-        store(2, every, "vector")
+        store(2, halves[0], "vector")
+        store(2, halves[1], "vector")
         store(3, halves[0], "scalar")
         store(3, halves[1], "scalar")

@@ -111,9 +111,9 @@ def tile_attend_gvq_s_x_kernel(tc, zT, cb, dyT, wm, offs, out):
                 in_=g_bf[g][:, tok, :].rearrange("p t j -> p (t j)"),
             )
 
-        def rounded_tile(g, first, last):
+        def rounded_tile(g, first, last, tag=None):
             name = "w_bf%d_%d" % (g, first)
-            tile = keep.tile([P, (last - first + 1) * P, PACK], BF16, name=name, tag=name, align_bytes=64)
+            tile = keep.tile([P, (last - first + 1) * P, PACK], BF16, name=name, tag=tag or name, align_bytes=64)
             for m in range(first, last + 1):
                 w_bf[g, m] = (tile, first)
 
@@ -156,6 +156,22 @@ def tile_attend_gvq_s_x_kernel(tc, zT, cb, dyT, wm, offs, out):
             for m in range(first, last + 1):
                 multiply(g, m)
 
+        def load_w_planes(pair, first, last):
+            src = rows(wm, 0)[:, 2 * pair : 2 * pair + 2, cols(first, last)]
+            tile = load("w_planes%d_%d" % (pair, first), src)
+            for m in range(first, last + 1):
+                ws["planes", pair, m] = (tile, first)
+
+        def round_w_planes(pair, first, last, engine):
+            tile, base = ws["planes", pair, first]
+            src = planar(tile[:, :, cols(first - base, last - base)])
+            tile, base = w_bf[0, first]
+            dst = packed(tile[:, cols(first - base, last - base), 2 * pair : 2 * pair + 2])
+            if engine == "scalar":
+                nc.scalar.copy(dst, src)
+            else:
+                nc.vector.tensor_copy(dst, src)
+
         def store(m, tok, engine):
             res = keep.tile([P, tok.stop - tok.start], F32, name="res%d_%d" % (m, tok.start))
             if engine == "scalar":
@@ -174,8 +190,10 @@ def tile_attend_gvq_s_x_kernel(tc, zT, cb, dyT, wm, offs, out):
         for r in range(4, 8):
             load_book(r, 1)
         load_z(1)
-        load_w(0, 0, 3)
+        load_w_planes(0, 0, 3)
+        load_w_planes(1, 0, 1)
         load_w(1, 0, 1)
+        load_w_planes(1, 2, 3)
         load_w(1, 2, 3)
 
         scale_dy(0, 2)
@@ -193,18 +211,24 @@ def tile_attend_gvq_s_x_kernel(tc, zT, cb, dyT, wm, offs, out):
         join_z(1, halves[0])
         join_z(1, halves[1])
         quantise_g(1, halves[0])
-        quantise_g(1, halves[1])
-        rounded_tile(0, 0, 3)
+        rounded_tile(0, 0, 1)
         for m in range(4):
             rounded_tile(1, m, m)
-            round_w(0, m, m, "scalar")
+        round_w_planes(0, 0, 1, "scalar")
+        round_w_planes(1, 0, 0, "scalar")
+        round_w_planes(1, 1, 1, "scalar")
+        rounded_tile(0, 2, 3, "w_planes1_0")
+        round_w_planes(0, 2, 3, "scalar")
         block(0, 0, 0)
+        quantise_g(1, halves[1])
         block(0, 1, 1)
         round_w(1, 0, 0, "vector")
         round_w(1, 1, 1, "vector")
         block(1, 0, 0)
         block(1, 1, 1)
-        block(0, 2, 3, "w_bf1_0")
+        round_w_planes(1, 2, 2, "scalar")
+        round_w_planes(1, 3, 3, "vector")
+        block(0, 2, 3)
         round_w(1, 2, 2, "vector")
         round_w(1, 3, 3, "vector")
         block(1, 2, 2)

@@ -180,25 +180,23 @@ def tile_attend_gvq_s_x_kernel(tc, zT, cb, dyT, wm, offs, out):
                 nc.vector.tensor_scalar_mul(res[:], banks[m][:, tok], BETA)
             nc.sync.dma_start(out=out[m * P : (m + 1) * P, tok], in_=res[:])
 
-        load_dy(0, 2)
+        load_dy(0, 4)
         nc.sync.dma_start(offsets[:], offs)
         load_book(0, 2)
-        load_dy(2, 2)
         load_book(2, 2)
         load_z(0)
         load_dy(4, 4)
         for r in range(4, 8):
             load_book(r, 1)
         load_z(1)
-        load_w_planes(0, 0, 3)
         load_w_planes(1, 0, 1)
+        load_w_planes(0, 0, 3)
         load_w(1, 0, 1)
         load_w_planes(1, 2, 3)
         load_w(1, 2, 3)
-
         scale_dy(0, 2)
-        move_book(1, 0)
         scale_dy(2, 2)
+        move_book(1, 0)
         move_book(3, 2)
         for r in range(4):
             gather(r)
@@ -214,16 +212,16 @@ def tile_attend_gvq_s_x_kernel(tc, zT, cb, dyT, wm, offs, out):
         rounded_tile(0, 0, 1)
         for m in range(4):
             rounded_tile(1, m, m)
-        round_w_planes(0, 0, 1, "scalar")
-        round_w_planes(1, 0, 0, "scalar")
-        round_w_planes(1, 1, 1, "scalar")
-        rounded_tile(0, 2, 3, "w_planes1_0")
+        round_w_planes(1, 0, 1, "scalar")
+        round_w_planes(0, 0, 0, "scalar")
+        round_w_planes(0, 1, 1, "scalar")
+        rounded_tile(0, 2, 3)
         round_w_planes(0, 2, 3, "scalar")
         block(0, 0, 0)
         quantise_g(1, halves[1])
         block(0, 1, 1)
         round_w(1, 0, 0, "vector")
-        round_w(1, 1, 1, "vector")
+        round_w(1, 1, 1, "scalar")
         block(1, 0, 0)
         block(1, 1, 1)
         round_w_planes(1, 2, 2, "scalar")

@@ -226,7 +226,8 @@ def tile_attend_gvq_s_x_kernel(tc, zT, cb, dyT, wm, offs, out):
         block(1, 1, 1)
         round_w_planes(1, 2, 2, "scalar")
         round_w_planes(1, 3, 3, "vector")
-        block(0, 2, 3)
+        block(0, 2, 2)
+        block(0, 3, 3)
         round_w(1, 2, 2, "vector")
         round_w(1, 3, 3, "vector")
         block(1, 2, 2)

@@ -127,6 +127,15 @@ def tile_attend_gvq_s_x_kernel(tc, zT, cb, dyT, wm, offs, out):
             else:
                 nc.vector.tensor_copy(dst, src)
 
+        def round_w_shared(g, m):
+            tile, base = ws[g, m]
+            out_tile, out_base = w_bf[g, m]
+            for part, copy in enumerate((nc.vector.tensor_copy, nc.scalar.copy)):
+                lo = part * P // 2
+                src = slice((m - base) * P + lo, (m - base) * P + lo + P // 2)
+                dst = slice((m - out_base) * P + lo, (m - out_base) * P + lo + P // 2)
+                copy(packed(out_tile[:, dst, :]), planar(tile[:, :, src]))
+
         def quantise_w(g, first, last, tag):
             name = "w_codes%d_%d" % (g, first)
             codes = keep.tile([P, (last - first + 1) * P], U32, name=name, tag=tag or name, align_bytes=64)
@@ -156,21 +165,40 @@ def tile_attend_gvq_s_x_kernel(tc, zT, cb, dyT, wm, offs, out):
             for m in range(first, last + 1):
                 multiply(g, m)
 
-        def load_w_planes(pair, first, last):
-            src = rows(wm, 0)[:, 2 * pair : 2 * pair + 2, cols(first, last)]
-            tile = load("w_planes%d_%d" % (pair, first), src)
+        def load_w_planes(pair, first, last, g=0):
+            src = rows(wm, g)[:, 2 * pair : 2 * pair + 2, cols(first, last)]
+            tile = load("w_planes%d_%d_%d" % (g, pair, first), src)
             for m in range(first, last + 1):
-                ws["planes", pair, m] = (tile, first)
+                ws["planes", g, pair, m] = (tile, first)
 
-        def round_w_planes(pair, first, last, engine):
-            tile, base = ws["planes", pair, first]
+        def round_w_planes(pair, first, last, engine, g=0):
+            tile, base = ws["planes", g, pair, first]
             src = planar(tile[:, :, cols(first - base, last - base)])
-            tile, base = w_bf[0, first]
+            tile, base = w_bf[g, first]
             dst = packed(tile[:, cols(first - base, last - base), 2 * pair : 2 * pair + 2])
             if engine == "scalar":
                 nc.scalar.copy(dst, src)
             else:
                 nc.vector.tensor_copy(dst, src)
+
+        def load_w_front():
+            tile = keep.tile([P, PACK, D], F32, name="w_front", align_bytes=64)
+            run = slice(0, D + D // 2)
+            nc.sync.dma_start(
+                out=tile[:].rearrange("p (q i) d -> p q (i d)", i=2)[:, :, run],
+                in_=rows(wm, 0).rearrange("p (q i) d -> p q (i d)", i=2)[:, :, run],
+            )
+            for m in range(4):
+                ws[0, m] = (tile, 0)
+
+        def load_w_rest():
+            ws["rest"] = load("w_rest", rows(wm, 0)[:, 1::2, cols(2, 3)])
+
+        def round_w_high(m, copy):
+            tile, base = w_bf[0, m]
+            dst = tile[:, cols(m - base, m - base), :]
+            copy(packed(dst[:, :, 0::2]), planar(ws[0, m][0][:, 0::2, cols(m, m)]))
+            copy(packed(dst[:, :, 1::2]), planar(ws["rest"][:, :, cols(m - 2, m - 2)]))
 
         def store(m, tok, engine):
             res = keep.tile([P, tok.stop - tok.start], F32, name="res%d_%d" % (m, tok.start))
@@ -189,11 +217,11 @@ def tile_attend_gvq_s_x_kernel(tc, zT, cb, dyT, wm, offs, out):
         for r in range(4, 8):
             load_book(r, 1)
         load_z(1)
-        load_w_planes(1, 0, 1)
-        load_w_planes(0, 0, 3)
+        load_w_front()
         load_w(1, 0, 1)
-        load_w_planes(1, 2, 3)
-        load_w(1, 2, 3)
+        load_w_rest()
+        load_w_planes(0, 2, 3, 1)
+        load_w_planes(1, 2, 3, 1)
         scale_dy(0, 2)
         scale_dy(2, 2)
         move_book(1, 0)
@@ -210,31 +238,32 @@ def tile_attend_gvq_s_x_kernel(tc, zT, cb, dyT, wm, offs, out):
         join_z(1, halves[1])
         quantise_g(1, halves[0])
         rounded_tile(0, 0, 1)
-        for m in range(4):
+        for m in range(2):
             rounded_tile(1, m, m)
-        round_w_planes(1, 0, 1, "scalar")
-        round_w_planes(0, 0, 0, "scalar")
-        round_w_planes(0, 1, 1, "scalar")
-        rounded_tile(0, 2, 3)
-        round_w_planes(0, 2, 3, "scalar")
+        rounded_tile(1, 2, 3)
+        round_w(0, 0, 0, "scalar")
+        round_w(0, 1, 1, "scalar")
         block(0, 0, 0)
         quantise_g(1, halves[1])
         block(0, 1, 1)
-        round_w(1, 0, 0, "vector")
-        round_w(1, 1, 1, "scalar")
+        round_w_shared(1, 0)
+        round_w_shared(1, 1)
         block(1, 0, 0)
         block(1, 1, 1)
-        round_w_planes(1, 2, 2, "scalar")
-        round_w_planes(1, 3, 3, "vector")
+        rounded_tile(0, 2, 3, "w1_0")
+        round_w_high(2, nc.scalar.copy)
+        round_w_high(3, nc.vector.tensor_copy)
         block(0, 2, 2)
         block(0, 3, 3)
-        round_w(1, 2, 2, "vector")
-        round_w(1, 3, 3, "vector")
+        round_w_planes(0, 2, 3, "vector", 1)
+        round_w_planes(1, 2, 2, "vector", 1)
+        round_w_planes(1, 3, 3, "vector", 1)
         block(1, 2, 2)
         block(1, 3, 3)
         store(0, halves[0], "scalar")
         store(0, halves[1], "scalar")
-        store(1, every, "scalar")
+        store(1, halves[0], "scalar")
+        store(1, halves[1], "scalar")
         store(2, halves[0], "vector")
         store(2, halves[1], "vector")
         store(3, halves[0], "scalar")

@@ -183,16 +183,24 @@ def tile_attend_gvq_s_x_kernel(tc, zT, cb, dyT, wm, offs, out):
 
         def load_w_front():
             tile = keep.tile([P, PACK, D], F32, name="w_front", align_bytes=64)
-            run = slice(0, D + D // 2)
-            nc.sync.dma_start(
-                out=tile[:].rearrange("p (q i) d -> p q (i d)", i=2)[:, :, run],
-                in_=rows(wm, 0).rearrange("p (q i) d -> p q (i d)", i=2)[:, :, run],
-            )
+            for pair in (1, 0):
+                run = slice(2 * pair * D, (2 * pair + 1) * D + D // 2)
+                nc.sync.dma_start(
+                    out=tile[:].rearrange("p j d -> p (j d)")[:, run],
+                    in_=rows(wm, 0).rearrange("p j d -> p (j d)")[:, run],
+                )
             for m in range(4):
                 ws[0, m] = (tile, 0)
 
         def load_w_rest():
             ws["rest"] = load("w_rest", rows(wm, 0)[:, 1::2, cols(2, 3)])
+
+        def round_w_low(first, last, pair):
+            planes = slice(2 * pair, 2 * pair + 2)
+            nc.scalar.copy(
+                packed(w_bf[0, first][0][:, cols(first, last), planes]),
+                planar(ws[0, first][0][:, planes, cols(first, last)]),
+            )
 
         def round_w_high(m, copy):
             tile, base = w_bf[0, m]
@@ -220,8 +228,7 @@ def tile_attend_gvq_s_x_kernel(tc, zT, cb, dyT, wm, offs, out):
         load_w_front()
         load_w(1, 0, 1)
         load_w_rest()
-        load_w_planes(0, 2, 3, 1)
-        load_w_planes(1, 2, 3, 1)
+        load_w(1, 2, 3)
         scale_dy(0, 2)
         scale_dy(2, 2)
         move_book(1, 0)
@@ -238,16 +245,17 @@ def tile_attend_gvq_s_x_kernel(tc, zT, cb, dyT, wm, offs, out):
         join_z(1, halves[1])
         quantise_g(1, halves[0])
         rounded_tile(0, 0, 1)
-        for m in range(2):
+        for m in range(4):
             rounded_tile(1, m, m)
-        rounded_tile(1, 2, 3)
-        round_w(0, 0, 0, "scalar")
-        round_w(0, 1, 1, "scalar")
+        round_w_low(0, 1, 1)
+        round_w_low(0, 0, 0)
+        round_w_low(1, 1, 0)
+        quantise_g(1, slice(HALF, HALF + P))
         block(0, 0, 0)
-        quantise_g(1, halves[1])
+        quantise_g(1, slice(HALF + P, T))
         block(0, 1, 1)
-        round_w_shared(1, 0)
-        round_w_shared(1, 1)
+        round_w(1, 0, 0, "vector")
+        round_w(1, 1, 1, "scalar")
         block(1, 0, 0)
         block(1, 1, 1)
         rounded_tile(0, 2, 3, "w1_0")
@@ -255,9 +263,8 @@ def tile_attend_gvq_s_x_kernel(tc, zT, cb, dyT, wm, offs, out):
         round_w_high(3, nc.vector.tensor_copy)
         block(0, 2, 2)
         block(0, 3, 3)
-        round_w_planes(0, 2, 3, "vector", 1)
-        round_w_planes(1, 2, 2, "vector", 1)
-        round_w_planes(1, 3, 3, "vector", 1)
+        round_w(1, 2, 2, "vector")
+        round_w(1, 3, 3, "vector")
         block(1, 2, 2)
         block(1, 3, 3)
         store(0, halves[0], "scalar")
@@ -266,5 +273,4 @@ def tile_attend_gvq_s_x_kernel(tc, zT, cb, dyT, wm, offs, out):
         store(1, halves[1], "scalar")
         store(2, halves[0], "vector")
         store(2, halves[1], "vector")
-        store(3, halves[0], "scalar")
-        store(3, halves[1], "scalar")
+        store(3, every, "scalar")

@@ -13,8 +13,6 @@ U16 = mybir.dt.uint16
 U8 = mybir.dt.uint8
 E4M3 = mybir.dt.float8_e4m3fn_x4
 E5M2 = mybir.dt.float8_e5m2_x4
-MULT = mybir.AluOpType.mult
-ADD = mybir.AluOpType.add
 SUB = mybir.AluOpType.subtract
 COPY = mybir.ActivationFunctionType.Copy
 
@@ -22,8 +20,15 @@ P = 128
 PACK = 4
 K_PASS = P * PACK
 PASSES = DV // K_PASS
-HALF = T // 2
+BLOCKS = D // P
+LIST_ROWS = 16
 RUN = 2
+HALF_T = T // 2
+HALF_D = D // 2
+
+RUN_UNITS = 3
+ODD_STEP = 5
+UNITS = 2 * ODD_STEP
 
 
 def planar(ap):
@@ -34,243 +39,180 @@ def packed(ap):
     return ap.rearrange("p (c i) j -> p c j i", i=RUN)
 
 
+def blocks(first, last):
+    return slice(first * P, (last + 1) * P)
+
+
 def tile_attend_gvq_s_x_kernel(tc, zT, cb, dyT, wm, offs, out):
     nc = tc.nc
 
-    def rows(x, g):
-        return x[g * K_PASS : (g + 1) * K_PASS, :].rearrange("(p j) w -> p j w", j=PACK)
+    def rows(x, s):
+        return x[s * K_PASS : (s + 1) * K_PASS, :].rearrange("(p j) w -> p j w", j=PACK)
 
     with ExitStack() as ctx:
         keep = ctx.enter_context(tc.tile_pool(name="keep", bufs=1))
         psum = ctx.enter_context(tc.psum_pool(name="psum", bufs=1))
 
-        offsets = keep.tile([P, T // 16], U16, name="offsets")
-        g_codes = {1: keep.tile([P, T], U32, name="g_codes1", align_bytes=64)}
-        g_scales = [keep.tile([P, T], U8, name="g_scales%d" % g, align_bytes=64) for g in range(PASSES)]
-        w_scales = keep.tile([P, PASSES, D], U8, name="w_scales", align_bytes=64)
-        banks = [psum.tile([P, T], F32, name="bank%d" % m) for m in range(D // P)]
-        parts = [keep.tile([P, PACK, T], F32, name="part%d" % g, align_bytes=64) for g in range(PASSES)]
-        g_bf = [keep.tile([P, T, PACK], BF16, name="g_bf%d" % g, align_bytes=64) for g in range(PASSES)]
-        halves = [slice(0, HALF), slice(HALF, T)]
-        every = slice(0, T)
-        books, dys, zs, ws, w_bf, w_codes = {}, {}, {}, {}, {}, {}
-
-        def clock(name, ap):
-            t = keep.tile([P, 1], ap.dtype, name=name)
-            nc.gpsimd.tensor_copy(t[:], ap)
+        def sbuf(name, shape, dtype):
+            return keep.tile(shape, dtype, name=name, align_bytes=64)
 
         def load(name, src):
-            tile = keep.tile(list(src.shape), F32, name=name, tag=name, align_bytes=64)
+            tile = sbuf(name, list(src.shape), F32)
             nc.sync.dma_start(out=tile[:], in_=src)
             return tile
 
-        def cols(first, last):
-            return slice(first * P, (last + 1) * P)
+        offsets = keep.tile([P, T // LIST_ROWS], U16, name="offsets")
+        g_codes = [sbuf("g_codes%d" % s, [P, T], U32) for s in range(PASSES)]
+        g_scales = [sbuf("g_scales%d" % s, [P, T], U8) for s in range(PASSES)]
+        w_scales = sbuf("w_scales", [P, PASSES, D], U8)
+        banks = [psum.tile([P, T], F32, name="bank%d" % m) for m in range(BLOCKS)]
+        picked = [sbuf("picked%d" % s, [P, PACK, T], F32) for s in range(PASSES)]
+        g_bf = [sbuf("g_bf%d" % s, [P, T, PACK], BF16) for s in range(PASSES)]
+        w0_low_bf = sbuf("w0_low_bf", [P, HALF_D, PACK], BF16)
+        w0_high_bf = sbuf("w0_high_bf", [P, HALF_D, PACK], BF16)
+        w1_bf = [sbuf("w1_bf%d" % m, [P, P, PACK], BF16) for m in range(BLOCKS)]
+        w_bf = [
+            [(w0_low_bf if m < 2 else w0_high_bf)[:, blocks(m % 2, m % 2), :] for m in range(BLOCKS)],
+            [tile[:] for tile in w1_bf],
+        ]
+        first_half, second_half = slice(0, HALF_T), slice(HALF_T, T)
+        books = {}
 
-        def load_book(r, n):
-            src = rows(cb, r // PACK)[:, r % PACK : r % PACK + n, :].rearrange("p j c -> p (j c)")
-            books[r] = load("book%d" % r, src)
+        def load_book(s, j, planes):
+            src = rows(cb, s)[:, j : j + planes, :].rearrange("p j c -> p (j c)")
+            books[s, j] = load("book%d_%d" % (s, j), src)
 
-        def move_book(r, source):
-            books[r] = keep.tile([P, C], F32, name="book%d" % r, tag="book%d" % r, align_bytes=64)
-            nc.scalar.activation(books[r][:], books[source][:, (r - source) * C : (r - source + 1) * C], COPY)
+        dy0 = load("dy0", rows(dyT, 0))
+        nc.sync.dma_start(offsets[:], offs)
+        load_book(0, 0, 2)
+        load_book(0, 2, 2)
+        z0 = load("z0", rows(zT, 0))
+        dy1 = load("dy1", rows(dyT, 1))
+        for j in range(PACK):
+            load_book(1, j, 1)
+        z1 = load("z1", rows(zT, 1))
+        dy, z = (dy0, dy1), (z0, z1)
 
-        def load_dy(r, n):
-            tile = load("dy%d" % r, rows(dyT, r // PACK)[:, r % PACK : r % PACK + n, :])
-            for i in range(n):
-                dys[r + i] = (tile, r)
+        w0 = sbuf("w0", [P, UNITS, HALF_D], F32)
+        w0_flat = rows(wm, 0).rearrange("p j d -> p (j d)")
+        for pair in (1, 0):
+            start = 2 * pair * D
+            nc.sync.dma_start(
+                out=w0[:, RUN_UNITS * pair : RUN_UNITS * (pair + 1), :].rearrange("p u d -> p (u d)"),
+                in_=w0_flat[:, start : start + RUN_UNITS * HALF_D],
+            )
+        w1_low = load("w1_low", rows(wm, 1)[:, :, :HALF_D])
+        nc.sync.dma_start(out=w0[:, 1 + ODD_STEP :: RUN_UNITS, :], in_=rows(wm, 0)[:, 1::2, HALF_D:])
+        w1_high = load("w1_high", rows(wm, 1)[:, :, HALF_D:])
 
-        def load_z(g):
-            zs[g] = load("z%d" % g, rows(zT, g))
+        def scale_dy(s, j, planes):
+            part = dy[s][:, j : j + planes, :]
+            nc.scalar.activation(part, part, COPY, scale=1.0 / BETA)
 
-        def load_w(g, first, last):
-            tile = load("w%d_%d" % (g, first), rows(wm, g)[:, :, cols(first, last)])
-            for m in range(first, last + 1):
-                ws[g, m] = (tile, first)
+        def move_book(s, j):
+            books[s, j] = sbuf("book%d_%d" % (s, j), [P, C], F32)
+            nc.scalar.activation(books[s, j][:], books[s, j - 1][:, C:], COPY)
 
-        def scale_dy(r, n):
-            dy, first = dys[r]
-            planes = dy[:, r - first : r - first + n, :]
-            nc.scalar.activation(planes, planes, COPY, scale=1.0 / BETA)
+        def gather(s, j):
+            nc.vector.tensor_tensor(picked[s][:, j, :], books[s, j][:].indirect(offsets[:]), dy[s][:, j, :], SUB)
 
-        def gather(r):
-            dy, first = dys[r]
+        def join_z(s, tok):
             nc.vector.tensor_tensor(
-                parts[r // PACK][:, r % PACK, :], books[r][:].indirect(offsets[:]), dy[:, r - first, :], SUB
+                packed(g_bf[s][:, tok, :]), planar(z[s][:, :, tok]), planar(picked[s][:, :, tok]), SUB
             )
 
-        def join_z(g, tok):
-            nc.vector.tensor_tensor(
-                packed(g_bf[g][:, tok, :]), planar(zs[g][:, :, tok]), planar(parts[g][:, :, tok]), SUB
-            )
-
-        def quantise_g(g, tok):
+        def quantise_g(s, tok):
             nc.vector.quantize_mx(
-                out=g_codes[g][:, tok].bitcast(E5M2),
-                scales=g_scales[g][:, tok],
-                in_=g_bf[g][:, tok, :].rearrange("p t j -> p (t j)"),
+                out=g_codes[s][:, tok].bitcast(E5M2),
+                scales=g_scales[s][:, tok],
+                in_=g_bf[s][:, tok, :].rearrange("p t j -> p (t j)"),
             )
 
-        def rounded_tile(g, first, last, tag=None):
-            name = "w_bf%d_%d" % (g, first)
-            tile = keep.tile([P, (last - first + 1) * P, PACK], BF16, name=name, tag=tag or name, align_bytes=64)
-            for m in range(first, last + 1):
-                w_bf[g, m] = (tile, first)
+        def round_w0_low(first, last, pair):
+            units = slice(RUN_UNITS * pair, RUN_UNITS * (pair + 1), RUN_UNITS - 1)
+            nc.scalar.copy(
+                packed(w0_low_bf[:, blocks(first, last), 2 * pair : 2 * pair + 2]),
+                planar(w0[:, units, blocks(first, last)]),
+            )
 
-        def round_w(g, first, last, engine):
-            tile, base = ws[g, first]
-            src = planar(tile[:, :, cols(first - base, last - base)])
-            tile, base = w_bf[g, first]
-            dst = packed(tile[:, cols(first - base, last - base), :])
-            if engine == "scalar":
-                nc.scalar.copy(dst, src)
-            else:
-                nc.vector.tensor_copy(dst, src)
+        def round_w0_high(m, copy):
+            units = w0[:].rearrange("p (i u) d -> p i u d", i=2)[:, :, 1:ODD_STEP:RUN_UNITS, blocks(m - 2, m - 2)]
+            copy(
+                w_bf[0][m].rearrange("p (c r) (q i) -> p c q i r", r=RUN, i=2),
+                units.rearrange("p i q (c r) -> p c q i r", r=RUN),
+            )
 
-        def round_w_shared(g, m):
-            tile, base = ws[g, m]
-            out_tile, out_base = w_bf[g, m]
-            for part, copy in enumerate((nc.vector.tensor_copy, nc.scalar.copy)):
-                lo = part * P // 2
-                src = slice((m - base) * P + lo, (m - base) * P + lo + P // 2)
-                dst = slice((m - out_base) * P + lo, (m - out_base) * P + lo + P // 2)
-                copy(packed(out_tile[:, dst, :]), planar(tile[:, :, src]))
+        def round_w1(m, copy):
+            half = w1_low if m < 2 else w1_high
+            copy(packed(w_bf[1][m]), planar(half[:, :, blocks(m % 2, m % 2)]))
 
-        def quantise_w(g, first, last, tag):
-            name = "w_codes%d_%d" % (g, first)
-            codes = keep.tile([P, (last - first + 1) * P], U32, name=name, tag=tag or name, align_bytes=64)
-            for m in range(first, last + 1):
-                w_codes[g, m] = codes[:, cols(m - first, m - first)]
-            tile, base = w_bf[g, first]
+        def multiply(s, m):
+            codes = sbuf("w_codes%d_%d" % (s, m), [P, P], U32)
+            scales = w_scales[:, s, blocks(m, m)]
             nc.vector.quantize_mx(
-                out=codes[:].bitcast(E4M3),
-                scales=w_scales[:, g, cols(first, last)],
-                in_=tile[:, cols(first - base, last - base), :].rearrange("p d j -> p (d j)"),
+                out=codes[:].bitcast(E4M3), scales=scales, in_=w_bf[s][m].rearrange("p d j -> p (d j)")
             )
-
-        def multiply(g, m):
-            span = cols(m, m)
             nc.tensor.matmul_mx(
                 out=banks[m][:],
-                lhsT=w_codes[g, m].bitcast(E4M3),
-                lhsT_scale=w_scales[:, g, span],
-                rhs=g_codes[g][:].bitcast(E5M2),
-                rhs_scale=g_scales[g][:],
-                start=(g == 0),
-                stop=(g == PASSES - 1),
+                lhsT=codes[:].bitcast(E4M3),
+                lhsT_scale=scales,
+                rhs=g_codes[s][:].bitcast(E5M2),
+                rhs_scale=g_scales[s][:],
+                start=(s == 0),
+                stop=(s == PASSES - 1),
             )
 
-        def block(g, first, last, tag=None):
-            quantise_w(g, first, last, tag)
-            for m in range(first, last + 1):
-                multiply(g, m)
+        def empty_on_scalar(res, src):
+            nc.scalar.activation(res, src, COPY, scale=BETA)
 
-        def load_w_planes(pair, first, last, g=0):
-            src = rows(wm, g)[:, 2 * pair : 2 * pair + 2, cols(first, last)]
-            tile = load("w_planes%d_%d_%d" % (g, pair, first), src)
-            for m in range(first, last + 1):
-                ws["planes", g, pair, m] = (tile, first)
+        def empty_on_vector(res, src):
+            nc.vector.tensor_scalar_mul(res, src, BETA)
 
-        def round_w_planes(pair, first, last, engine, g=0):
-            tile, base = ws["planes", g, pair, first]
-            src = planar(tile[:, :, cols(first - base, last - base)])
-            tile, base = w_bf[g, first]
-            dst = packed(tile[:, cols(first - base, last - base), 2 * pair : 2 * pair + 2])
-            if engine == "scalar":
-                nc.scalar.copy(dst, src)
-            else:
-                nc.vector.tensor_copy(dst, src)
-
-        def load_w_front():
-            tile = keep.tile([P, PACK, D], F32, name="w_front", align_bytes=64)
-            for pair in (1, 0):
-                run = slice(2 * pair * D, (2 * pair + 1) * D + D // 2)
-                nc.sync.dma_start(
-                    out=tile[:].rearrange("p j d -> p (j d)")[:, run],
-                    in_=rows(wm, 0).rearrange("p j d -> p (j d)")[:, run],
-                )
-            for m in range(4):
-                ws[0, m] = (tile, 0)
-
-        def load_w_rest():
-            ws["rest"] = load("w_rest", rows(wm, 0)[:, 1::2, cols(2, 3)])
-
-        def round_w_low(first, last, pair):
-            planes = slice(2 * pair, 2 * pair + 2)
-            nc.scalar.copy(
-                packed(w_bf[0, first][0][:, cols(first, last), planes]),
-                planar(ws[0, first][0][:, planes, cols(first, last)]),
-            )
-
-        def round_w_high(m, copy):
-            tile, base = w_bf[0, m]
-            dst = tile[:, cols(m - base, m - base), :]
-            copy(packed(dst[:, :, 0::2]), planar(ws[0, m][0][:, 0::2, cols(m, m)]))
-            copy(packed(dst[:, :, 1::2]), planar(ws["rest"][:, :, cols(m - 2, m - 2)]))
-
-        def store(m, tok, engine):
+        def store(m, tok, empty):
             res = keep.tile([P, tok.stop - tok.start], F32, name="res%d_%d" % (m, tok.start))
-            if engine == "scalar":
-                nc.scalar.activation(res[:], banks[m][:, tok], COPY, scale=BETA)
-            else:
-                nc.vector.tensor_scalar_mul(res[:], banks[m][:, tok], BETA)
-            nc.sync.dma_start(out=out[m * P : (m + 1) * P, tok], in_=res[:])
+            empty(res[:], banks[m][:, tok])
+            nc.sync.dma_start(out=out[blocks(m, m), tok], in_=res[:])
 
-        load_dy(0, 4)
-        nc.sync.dma_start(offsets[:], offs)
-        load_book(0, 2)
-        load_book(2, 2)
-        load_z(0)
-        load_dy(4, 4)
-        for r in range(4, 8):
-            load_book(r, 1)
-        load_z(1)
-        load_w_front()
-        load_w(1, 0, 1)
-        load_w_rest()
-        load_w(1, 2, 3)
-        scale_dy(0, 2)
-        scale_dy(2, 2)
-        move_book(1, 0)
-        move_book(3, 2)
-        for r in range(4):
-            gather(r)
-        join_z(0, every)
-        g_codes[0] = keep.tile([P, T], U32, name="g_codes0", align_bytes=64)
-        quantise_g(0, every)
-        for r in range(4, 8):
-            scale_dy(r, 1)
-            gather(r)
-        join_z(1, halves[0])
-        join_z(1, halves[1])
-        quantise_g(1, halves[0])
-        rounded_tile(0, 0, 1)
-        for m in range(4):
-            rounded_tile(1, m, m)
-        round_w_low(0, 1, 1)
-        round_w_low(0, 0, 0)
-        round_w_low(1, 1, 0)
-        quantise_g(1, slice(HALF, HALF + P))
-        block(0, 0, 0)
-        quantise_g(1, slice(HALF + P, T))
-        block(0, 1, 1)
-        round_w(1, 0, 0, "vector")
-        round_w(1, 1, 1, "scalar")
-        block(1, 0, 0)
-        block(1, 1, 1)
-        rounded_tile(0, 2, 3, "w1_0")
-        round_w_high(2, nc.scalar.copy)
-        round_w_high(3, nc.vector.tensor_copy)
-        block(0, 2, 2)
-        block(0, 3, 3)
-        round_w(1, 2, 2, "vector")
-        round_w(1, 3, 3, "vector")
-        block(1, 2, 2)
-        block(1, 3, 3)
-        store(0, halves[0], "scalar")
-        store(0, halves[1], "scalar")
-        store(1, halves[0], "scalar")
-        store(1, halves[1], "scalar")
-        store(2, halves[0], "vector")
-        store(2, halves[1], "vector")
-        store(3, every, "scalar")
+        for j in (0, 2):
+            scale_dy(0, j, 2)
+        for j in (1, 3):
+            move_book(0, j)
+        for j in range(PACK):
+            gather(0, j)
+        for tok in (first_half, second_half):
+            join_z(0, tok)
+        for tok in (first_half, second_half):
+            quantise_g(0, tok)
+
+        for j in range(PACK):
+            scale_dy(1, j, 1)
+            gather(1, j)
+        for tok in (first_half, second_half):
+            join_z(1, tok)
+        quantise_g(1, first_half)
+
+        round_w0_low(0, 1, 1)
+        round_w0_low(0, 0, 0)
+        round_w0_low(1, 1, 0)
+        quantise_g(1, slice(HALF_T, HALF_T + T // 4))
+        multiply(0, 0)
+        quantise_g(1, slice(HALF_T + T // 4, T))
+        multiply(0, 1)
+
+        round_w1(0, nc.vector.tensor_copy)
+        round_w1(1, nc.scalar.copy)
+        multiply(1, 0)
+        multiply(1, 1)
+        round_w0_high(2, nc.scalar.copy)
+        round_w0_high(3, nc.vector.tensor_copy)
+        multiply(0, 2)
+        multiply(0, 3)
+        round_w1(2, nc.vector.tensor_copy)
+        round_w1(3, nc.vector.tensor_copy)
+        multiply(1, 2)
+        multiply(1, 3)
+
+        for m, empty in ((0, empty_on_scalar), (1, empty_on_scalar), (2, empty_on_vector)):
+            for tok in (first_half, second_half):
+                store(m, tok, empty)
+        store(3, slice(0, T), empty_on_scalar)

@@ -65,7 +65,6 @@ def tile_attend_gvq_s_x_kernel(tc, zT, cb, dyT, wm, offs, out):
         g_codes = [sbuf("g_codes%d" % s, [P, T], U32) for s in range(PASSES)]
         g_scales = [sbuf("g_scales%d" % s, [P, T], U8) for s in range(PASSES)]
         w_scales = sbuf("w_scales", [P, PASSES, D], U8)
-        banks = [psum.tile([P, T], F32, name="bank%d" % m) for m in range(BLOCKS)]
         picked = [sbuf("picked%d" % s, [P, PACK, T], F32) for s in range(PASSES)]
         g_bf = [sbuf("g_bf%d" % s, [P, T, PACK], BF16) for s in range(PASSES)]
         w0_low_bf = sbuf("w0_low_bf", [P, HALF_D, PACK], BF16)
@@ -76,6 +75,11 @@ def tile_attend_gvq_s_x_kernel(tc, zT, cb, dyT, wm, offs, out):
             [tile[:] for tile in w1_bf],
         ]
         first_half, second_half = slice(0, HALF_T), slice(HALF_T, T)
+        pieces = [[slice(0, T)] if m < 3 else [first_half, second_half] for m in range(BLOCKS)]
+        banks = [
+            [psum.tile([P, tok.stop - tok.start], F32, name="bank%d_%d" % (m, tok.start)) for tok in pieces[m]]
+            for m in range(BLOCKS)
+        ]
         books = {}
 
         def load_book(s, j, planes):
@@ -103,7 +107,7 @@ def tile_attend_gvq_s_x_kernel(tc, zT, cb, dyT, wm, offs, out):
             )
         w1_low = load("w1_low", rows(wm, 1)[:, :, :HALF_D])
         nc.sync.dma_start(out=w0[:, 1 + ODD_STEP :: RUN_UNITS, :], in_=rows(wm, 0)[:, 1::2, HALF_D:])
-        w1_high = load("w1_high", rows(wm, 1)[:, :, HALF_D:])
+        w1_late = [load("w1_block%d" % m, rows(wm, 1)[:, :, blocks(m, m)]) for m in (2, 3)]
 
         def scale_dy(s, j, planes):
             part = dy[s][:, j : j + planes, :]
@@ -143,8 +147,8 @@ def tile_attend_gvq_s_x_kernel(tc, zT, cb, dyT, wm, offs, out):
             )
 
         def round_w1(m, copy):
-            half = w1_low if m < 2 else w1_high
-            copy(packed(w_bf[1][m]), planar(half[:, :, blocks(m % 2, m % 2)]))
+            src = w1_low[:, :, blocks(m, m)] if m < 2 else w1_late[m - 2][:]
+            copy(packed(w_bf[1][m]), planar(src))
 
         def multiply(s, m):
             codes = sbuf("w_codes%d_%d" % (s, m), [P, P], U32)
@@ -152,15 +156,16 @@ def tile_attend_gvq_s_x_kernel(tc, zT, cb, dyT, wm, offs, out):
             nc.vector.quantize_mx(
                 out=codes[:].bitcast(E4M3), scales=scales, in_=w_bf[s][m].rearrange("p d j -> p (d j)")
             )
-            nc.tensor.matmul_mx(
-                out=banks[m][:],
-                lhsT=codes[:].bitcast(E4M3),
-                lhsT_scale=scales,
-                rhs=g_codes[s][:].bitcast(E5M2),
-                rhs_scale=g_scales[s][:],
-                start=(s == 0),
-                stop=(s == PASSES - 1),
-            )
+            for bank, tok in zip(banks[m], pieces[m]):
+                nc.tensor.matmul_mx(
+                    out=bank[:],
+                    lhsT=codes[:].bitcast(E4M3),
+                    lhsT_scale=scales,
+                    rhs=g_codes[s][:, tok].bitcast(E5M2),
+                    rhs_scale=g_scales[s][:, tok],
+                    start=(s == 0),
+                    stop=(s == PASSES - 1),
+                )
 
         def empty_on_scalar(res, src):
             nc.scalar.activation(res, src, COPY, scale=BETA)
@@ -170,7 +175,7 @@ def tile_attend_gvq_s_x_kernel(tc, zT, cb, dyT, wm, offs, out):
 
         def store(m, tok, empty):
             res = keep.tile([P, tok.stop - tok.start], F32, name="res%d_%d" % (m, tok.start))
-            empty(res[:], banks[m][:, tok])
+            empty(res[:], banks[m][0][:, tok])
             nc.sync.dma_start(out=out[blocks(m, m), tok], in_=res[:])
 
         for j in (0, 2):
@@ -206,13 +211,16 @@ def tile_attend_gvq_s_x_kernel(tc, zT, cb, dyT, wm, offs, out):
         round_w0_high(2, nc.scalar.copy)
         round_w0_high(3, nc.vector.tensor_copy)
         multiply(0, 2)
-        multiply(0, 3)
         round_w1(2, nc.vector.tensor_copy)
-        round_w1(3, nc.vector.tensor_copy)
+        multiply(0, 3)
         multiply(1, 2)
+        round_w1(3, nc.vector.tensor_copy)
         multiply(1, 3)
 
-        for m, empty in ((0, empty_on_scalar), (1, empty_on_scalar), (2, empty_on_vector)):
+        for m in range(BLOCKS - 1):
             for tok in (first_half, second_half):
-                store(m, tok, empty)
-        store(3, slice(0, T), empty_on_scalar)
+                store(m, tok, empty_on_scalar)
+        last = keep.tile([P, T], F32, name="res3")
+        empty_on_vector(last[:, first_half], banks[3][0][:])
+        empty_on_scalar(last[:, second_half], banks[3][1][:])
+        nc.sync.dma_start(out=out[blocks(3, 3), :], in_=last[:])

@@ -8,12 +8,15 @@ FLOPS = 2 * DV * D * T
 
 F32 = mybir.dt.float32
 BF16 = mybir.dt.bfloat16
+I32 = mybir.dt.int32
 U32 = mybir.dt.uint32
 U16 = mybir.dt.uint16
 U8 = mybir.dt.uint8
 E4M3 = mybir.dt.float8_e4m3fn_x4
 E5M2 = mybir.dt.float8_e5m2_x4
+ADD = mybir.AluOpType.add
 SUB = mybir.AluOpType.subtract
+MULT = mybir.AluOpType.mult
 COPY = mybir.ActivationFunctionType.Copy
 
 P = 128
@@ -65,7 +68,8 @@ def tile_attend_gvq_s_x_kernel(tc, zT, cb, dyT, wm, offs, out):
         g_codes = [sbuf("g_codes%d" % s, [P, T], U32) for s in range(PASSES)]
         g_scales = [sbuf("g_scales%d" % s, [P, T], U8) for s in range(PASSES)]
         w_scales = sbuf("w_scales", [P, PASSES, D], U8)
-        picked = [sbuf("picked%d" % s, [P, PACK, T], F32) for s in range(PASSES)]
+        picked = [[sbuf("picked%d_%d" % (s, q), [P, 2, T], F32) for q in range(2)] for s in range(PASSES)]
+        g_pairs = sbuf("g_pairs", [P, 2, T, 2], BF16)
         g_bf = [sbuf("g_bf%d" % s, [P, T, PACK], BF16) for s in range(PASSES)]
         w0_low_bf = sbuf("w0_low_bf", [P, HALF_D, PACK], BF16)
         w0_high_bf = sbuf("w0_high_bf", [P, HALF_D, PACK], BF16)
@@ -75,27 +79,26 @@ def tile_attend_gvq_s_x_kernel(tc, zT, cb, dyT, wm, offs, out):
             [tile[:] for tile in w1_bf],
         ]
         first_half, second_half = slice(0, HALF_T), slice(HALF_T, T)
-        pieces = [[slice(0, T)] if m < 3 else [first_half, second_half] for m in range(BLOCKS)]
-        banks = [
-            [psum.tile([P, tok.stop - tok.start], F32, name="bank%d_%d" % (m, tok.start)) for tok in pieces[m]]
-            for m in range(BLOCKS)
-        ]
+        halves = (first_half, second_half)
+        banks = [[psum.tile([P, HALF_T], F32, name="bank%d_%d" % (m, h)) for h in range(2)] for m in range(BLOCKS)]
+        w_codes = [[sbuf("w_codes%d_%d" % (s, m), [P, P], U32) for m in range(BLOCKS)] for s in range(PASSES)]
         books = {}
 
         def load_book(s, j, planes):
             src = rows(cb, s)[:, j : j + planes, :].rearrange("p j c -> p (j c)")
             books[s, j] = load("book%d_%d" % (s, j), src)
 
-        dy0 = load("dy0", rows(dyT, 0))
-        nc.sync.dma_start(offsets[:], offs)
         load_book(0, 0, 2)
+        nc.sync.dma_start(offsets[:], offs)
         load_book(0, 2, 2)
+        dy0 = load("dy0", rows(dyT, 0))
         z0 = load("z0", rows(zT, 0))
-        dy1 = load("dy1", rows(dyT, 1))
-        for j in range(PACK):
-            load_book(1, j, 1)
-        z1 = load("z1", rows(zT, 1))
-        dy, z = (dy0, dy1), (z0, z1)
+        load_book(1, 0, 2)
+        load_book(1, 2, 2)
+        dy1, z1 = [], []
+        for q in range(2):
+            dy1.append(load("dy1_%d" % q, rows(dyT, 1)[:, 2 * q : 2 * q + 2, :]))
+            z1.append(load("z1_%d" % q, rows(zT, 1)[:, 2 * q : 2 * q + 2, :]))
 
         w0 = sbuf("w0", [P, UNITS, HALF_D], F32)
         w0_flat = rows(wm, 0).rearrange("p j d -> p (j d)")
@@ -109,21 +112,36 @@ def tile_attend_gvq_s_x_kernel(tc, zT, cb, dyT, wm, offs, out):
         nc.sync.dma_start(out=w0[:, 1 + ODD_STEP :: RUN_UNITS, :], in_=rows(wm, 0)[:, 1::2, HALF_D:])
         w1_late = [load("w1_block%d" % m, rows(wm, 1)[:, :, blocks(m, m)]) for m in (2, 3)]
 
-        def scale_dy(s, j, planes):
-            part = dy[s][:, j : j + planes, :]
-            nc.scalar.activation(part, part, COPY, scale=1.0 / BETA)
+        def gather_on_scalar(s, j):
+            nc.scalar.activation(picked[s][j // 2][:, j % 2, :], books[s, j][:].indirect(offsets[:]), COPY)
+
+        def gather_on_vector(s, j):
+            nc.vector.tensor_copy(picked[s][j // 2][:, j % 2, :], books[s, j - 1][:, C:].indirect(offsets[:]))
 
         def move_book(s, j):
             books[s, j] = sbuf("book%d_%d" % (s, j), [P, C], F32)
-            nc.scalar.activation(books[s, j][:], books[s, j - 1][:, C:], COPY)
+            nc.vector.tensor_copy(books[s, j][:], books[s, j - 1][:, C:])
 
-        def gather(s, j):
-            nc.vector.tensor_tensor(picked[s][:, j, :], books[s, j][:].indirect(offsets[:]), dy[s][:, j, :], SUB)
-
-        def join_z(s, tok):
-            nc.vector.tensor_tensor(
-                packed(g_bf[s][:, tok, :]), planar(z[s][:, :, tok]), planar(picked[s][:, :, tok]), SUB
+        def subtract(dy_pair, picked_pair, tok):
+            nc.vector.scalar_tensor_tensor(
+                dy_pair[:, :, tok], dy_pair[:, :, tok], 1.0 / BETA, picked_pair[:, :, tok], MULT, SUB
             )
+
+        def join_z0(tok):
+            nc.vector.tensor_tensor(packed(g_bf[0][:, tok, :]), planar(z0[:, :, tok]), planar(dy0[:, :, tok]), ADD)
+
+        def join_pair(q, tok):
+            nc.vector.tensor_tensor(
+                g_pairs[:, q, tok, :].rearrange("p (c i) j -> p c j i", i=2 * RUN),
+                z1[q][:, :, tok].rearrange("p j (c i) -> p c j i", i=2 * RUN),
+                dy1[q][:, :, tok].rearrange("p j (c i) -> p c j i", i=2 * RUN),
+                ADD,
+            )
+
+        def weave(tok):
+            words = g_pairs[:].rearrange("p q t j -> p q (t j)").bitcast(I32)
+            woven = g_bf[1][:].rearrange("p t j -> p (t j)").bitcast(I32).rearrange("p (t q) -> p t q", q=2)
+            nc.vector.tensor_copy(packed(woven[:, tok, :]), planar(words[:, :, tok]))
 
         def quantise_g(s, tok):
             nc.vector.quantize_mx(
@@ -150,17 +168,19 @@ def tile_attend_gvq_s_x_kernel(tc, zT, cb, dyT, wm, offs, out):
             src = w1_low[:, :, blocks(m, m)] if m < 2 else w1_late[m - 2][:]
             copy(packed(w_bf[1][m]), planar(src))
 
-        def multiply(s, m):
-            codes = sbuf("w_codes%d_%d" % (s, m), [P, P], U32)
-            scales = w_scales[:, s, blocks(m, m)]
+        def quantise_w(s, m):
             nc.vector.quantize_mx(
-                out=codes[:].bitcast(E4M3), scales=scales, in_=w_bf[s][m].rearrange("p d j -> p (d j)")
+                out=w_codes[s][m][:].bitcast(E4M3),
+                scales=w_scales[:, s, blocks(m, m)],
+                in_=w_bf[s][m].rearrange("p d j -> p (d j)"),
             )
-            for bank, tok in zip(banks[m], pieces[m]):
+
+        def multiply(s, m):
+            for bank, tok in zip(banks[m], halves):
                 nc.tensor.matmul_mx(
                     out=bank[:],
-                    lhsT=codes[:].bitcast(E4M3),
-                    lhsT_scale=scales,
+                    lhsT=w_codes[s][m][:].bitcast(E4M3),
+                    lhsT_scale=w_scales[:, s, blocks(m, m)],
                     rhs=g_codes[s][:, tok].bitcast(E5M2),
                     rhs_scale=g_scales[s][:, tok],
                     start=(s == 0),
@@ -173,54 +193,71 @@ def tile_attend_gvq_s_x_kernel(tc, zT, cb, dyT, wm, offs, out):
         def empty_on_vector(res, src):
             nc.vector.tensor_scalar_mul(res, src, BETA)
 
-        def store(m, tok, empty):
-            res = keep.tile([P, tok.stop - tok.start], F32, name="res%d_%d" % (m, tok.start))
-            empty(res[:], banks[m][0][:, tok])
-            nc.sync.dma_start(out=out[blocks(m, m), tok], in_=res[:])
+        def store_halves(m):
+            for h, tok in enumerate(halves):
+                res = keep.tile([P, HALF_T], F32, name="res%d_%d" % (m, h))
+                empty_on_scalar(res[:], banks[m][h][:])
+                nc.sync.dma_start(out=out[blocks(m, m), tok], in_=res[:])
+
+        def store_whole(m):
+            res = keep.tile([P, T], F32, name="res%d" % m)
+            empty_on_vector(res[:, first_half], banks[m][0][:])
+            empty_on_scalar(res[:, second_half], banks[m][1][:])
+            nc.sync.dma_start(out=out[blocks(m, m), :], in_=res[:])
 
         for j in (0, 2):
-            scale_dy(0, j, 2)
-        for j in (1, 3):
-            move_book(0, j)
-        for j in range(PACK):
-            gather(0, j)
-        for tok in (first_half, second_half):
-            join_z(0, tok)
-        for tok in (first_half, second_half):
+            gather_on_scalar(0, j)
+            gather_on_vector(0, j + 1)
+        for q in range(2):
+            subtract(dy0[:, 2 * q : 2 * q + 2, :], picked[0][q], slice(0, T))
+        for tok in halves:
+            join_z0(tok)
+        for tok in halves:
             quantise_g(0, tok)
 
-        for j in range(PACK):
-            scale_dy(1, j, 1)
-            gather(1, j)
-        for tok in (first_half, second_half):
-            join_z(1, tok)
+        gather_on_scalar(1, 0)
+        gather_on_vector(1, 1)
+        move_book(1, 3)
+        gather_on_scalar(1, 2)
+        gather_on_scalar(1, 3)
+        for q in range(2):
+            for tok in halves:
+                subtract(dy1[q], picked[1][q], tok)
+            for tok in halves:
+                join_pair(q, tok)
+        for tok in halves:
+            weave(tok)
         quantise_g(1, first_half)
 
         round_w0_low(0, 1, 1)
         round_w0_low(0, 0, 0)
         round_w0_low(1, 1, 0)
         quantise_g(1, slice(HALF_T, HALF_T + T // 4))
+        quantise_w(0, 0)
         multiply(0, 0)
         quantise_g(1, slice(HALF_T + T // 4, T))
+        quantise_w(0, 1)
         multiply(0, 1)
 
         round_w1(0, nc.vector.tensor_copy)
         round_w1(1, nc.scalar.copy)
+        quantise_w(1, 0)
         multiply(1, 0)
+        quantise_w(1, 1)
         multiply(1, 1)
         round_w0_high(2, nc.scalar.copy)
         round_w0_high(3, nc.vector.tensor_copy)
+        quantise_w(0, 2)
         multiply(0, 2)
         round_w1(2, nc.vector.tensor_copy)
-        multiply(0, 3)
+        quantise_w(0, 3)
+        quantise_w(1, 2)
         multiply(1, 2)
+        multiply(0, 3)
         round_w1(3, nc.vector.tensor_copy)
+        quantise_w(1, 3)
         multiply(1, 3)
 
         for m in range(BLOCKS - 1):
-            for tok in (first_half, second_half):
-                store(m, tok, empty_on_scalar)
-        last = keep.tile([P, T], F32, name="res3")
-        empty_on_vector(last[:, first_half], banks[3][0][:])
-        empty_on_scalar(last[:, second_half], banks[3][1][:])
-        nc.sync.dma_start(out=out[blocks(3, 3), :], in_=last[:])
+            store_halves(m)
+        store_whole(3)

from contextlib import ExitStack

import concourse.mybir as mybir

T, C, D, DV = 512, 1024, 512, 1024
BETA = 0.25
FLOPS = 2 * DV * D * T

F32 = mybir.dt.float32
BF16 = mybir.dt.bfloat16
I32 = mybir.dt.int32
U32 = mybir.dt.uint32
U16 = mybir.dt.uint16
U8 = mybir.dt.uint8
E4M3 = mybir.dt.float8_e4m3fn_x4
E5M2 = mybir.dt.float8_e5m2_x4
ADD = mybir.AluOpType.add
SUB = mybir.AluOpType.subtract
MULT = mybir.AluOpType.mult
COPY = mybir.ActivationFunctionType.Copy

P = 128
PACK = 4
K_PASS = P * PACK
PASSES = DV // K_PASS
BLOCKS = D // P
LIST_ROWS = 16
RUN = 2
HALF_T = T // 2
HALF_D = D // 2

RUN_UNITS = 3
ODD_STEP = 5
UNITS = 2 * ODD_STEP


def planar(ap):
    return ap.rearrange("p j (c i) -> p c j i", i=RUN)


def packed(ap):
    return ap.rearrange("p (c i) j -> p c j i", i=RUN)


def blocks(first, last):
    return slice(first * P, (last + 1) * P)


def tile_attend_gvq_s_x_kernel(tc, zT, cb, dyT, wm, offs, out):
    nc = tc.nc

    def rows(x, s):
        return x[s * K_PASS : (s + 1) * K_PASS, :].rearrange("(p j) w -> p j w", j=PACK)

    with ExitStack() as ctx:
        keep = ctx.enter_context(tc.tile_pool(name="keep", bufs=1))
        psum = ctx.enter_context(tc.psum_pool(name="psum", bufs=1))

        def sbuf(name, shape, dtype):
            return keep.tile(shape, dtype, name=name, align_bytes=64)

        def load(name, src):
            tile = sbuf(name, list(src.shape), F32)
            nc.sync.dma_start(out=tile[:], in_=src)
            return tile

        offsets = keep.tile([P, T // LIST_ROWS], U16, name="offsets")
        g_codes = [sbuf("g_codes%d" % s, [P, T], U32) for s in range(PASSES)]
        g_scales = [sbuf("g_scales%d" % s, [P, T], U8) for s in range(PASSES)]
        w_scales = sbuf("w_scales", [P, PASSES, D], U8)
        picked = [[sbuf("picked%d_%d" % (s, q), [P, 2, T], F32) for q in range(2)] for s in range(PASSES)]
        g_pairs = sbuf("g_pairs", [P, 2, T, 2], BF16)
        g_bf = [sbuf("g_bf%d" % s, [P, T, PACK], BF16) for s in range(PASSES)]
        w0_low_bf = sbuf("w0_low_bf", [P, HALF_D, PACK], BF16)
        w0_high_bf = sbuf("w0_high_bf", [P, HALF_D, PACK], BF16)
        w1_bf = [sbuf("w1_bf%d" % m, [P, P, PACK], BF16) for m in range(BLOCKS)]
        w_bf = [
            [(w0_low_bf if m < 2 else w0_high_bf)[:, blocks(m % 2, m % 2), :] for m in range(BLOCKS)],
            [tile[:] for tile in w1_bf],
        ]
        first_half, second_half = slice(0, HALF_T), slice(HALF_T, T)
        halves = (first_half, second_half)
        banks = [[psum.tile([P, HALF_T], F32, name="bank%d_%d" % (m, h)) for h in range(2)] for m in range(BLOCKS)]
        w_codes = [[sbuf("w_codes%d_%d" % (s, m), [P, P], U32) for m in range(BLOCKS)] for s in range(PASSES)]
        books = {}

        def load_book(s, j, planes):
            src = rows(cb, s)[:, j : j + planes, :].rearrange("p j c -> p (j c)")
            books[s, j] = load("book%d_%d" % (s, j), src)

        load_book(0, 0, 2)
        nc.sync.dma_start(offsets[:], offs)
        load_book(0, 2, 2)
        dy0 = load("dy0", rows(dyT, 0))
        z0 = load("z0", rows(zT, 0))
        load_book(1, 0, 2)
        load_book(1, 2, 2)
        dy1, z1 = [], []
        for q in range(2):
            dy1.append(load("dy1_%d" % q, rows(dyT, 1)[:, 2 * q : 2 * q + 2, :]))
            z1.append(load("z1_%d" % q, rows(zT, 1)[:, 2 * q : 2 * q + 2, :]))

        w0 = sbuf("w0", [P, UNITS, HALF_D], F32)
        w0_flat = rows(wm, 0).rearrange("p j d -> p (j d)")
        for pair in (1, 0):
            start = 2 * pair * D
            nc.sync.dma_start(
                out=w0[:, RUN_UNITS * pair : RUN_UNITS * (pair + 1), :].rearrange("p u d -> p (u d)"),
                in_=w0_flat[:, start : start + RUN_UNITS * HALF_D],
            )
        w1_low = load("w1_low", rows(wm, 1)[:, :, :HALF_D])
        nc.sync.dma_start(out=w0[:, 1 + ODD_STEP :: RUN_UNITS, :], in_=rows(wm, 0)[:, 1::2, HALF_D:])
        w1_late = [load("w1_block%d" % m, rows(wm, 1)[:, :, blocks(m, m)]) for m in (2, 3)]

        def gather_on_scalar(s, j):
            nc.scalar.activation(picked[s][j // 2][:, j % 2, :], books[s, j][:].indirect(offsets[:]), COPY)

        def gather_on_vector(s, j):
            nc.vector.tensor_copy(picked[s][j // 2][:, j % 2, :], books[s, j - 1][:, C:].indirect(offsets[:]))

        def move_book(s, j):
            books[s, j] = sbuf("book%d_%d" % (s, j), [P, C], F32)
            nc.vector.tensor_copy(books[s, j][:], books[s, j - 1][:, C:])

        def subtract(dy_pair, picked_pair, tok):
            nc.vector.scalar_tensor_tensor(
                dy_pair[:, :, tok], dy_pair[:, :, tok], 1.0 / BETA, picked_pair[:, :, tok], MULT, SUB
            )

        def join_z0(tok):
            nc.vector.tensor_tensor(packed(g_bf[0][:, tok, :]), planar(z0[:, :, tok]), planar(dy0[:, :, tok]), ADD)

        def join_pair(q, tok):
            nc.vector.tensor_tensor(
                g_pairs[:, q, tok, :].rearrange("p (c i) j -> p c j i", i=2 * RUN),
                z1[q][:, :, tok].rearrange("p j (c i) -> p c j i", i=2 * RUN),
                dy1[q][:, :, tok].rearrange("p j (c i) -> p c j i", i=2 * RUN),
                ADD,
            )

        def weave(tok):
            words = g_pairs[:].rearrange("p q t j -> p q (t j)").bitcast(I32)
            woven = g_bf[1][:].rearrange("p t j -> p (t j)").bitcast(I32).rearrange("p (t q) -> p t q", q=2)
            nc.vector.tensor_copy(packed(woven[:, tok, :]), planar(words[:, :, tok]))

        def quantise_g(s, tok):
            nc.vector.quantize_mx(
                out=g_codes[s][:, tok].bitcast(E5M2),
                scales=g_scales[s][:, tok],
                in_=g_bf[s][:, tok, :].rearrange("p t j -> p (t j)"),
            )

        def round_w0_low(first, last, pair):
            units = slice(RUN_UNITS * pair, RUN_UNITS * (pair + 1), RUN_UNITS - 1)
            nc.scalar.copy(
                packed(w0_low_bf[:, blocks(first, last), 2 * pair : 2 * pair + 2]),
                planar(w0[:, units, blocks(first, last)]),
            )

        def round_w0_high(m, copy):
            units = w0[:].rearrange("p (i u) d -> p i u d", i=2)[:, :, 1:ODD_STEP:RUN_UNITS, blocks(m - 2, m - 2)]
            copy(
                w_bf[0][m].rearrange("p (c r) (q i) -> p c q i r", r=RUN, i=2),
                units.rearrange("p i q (c r) -> p c q i r", r=RUN),
            )

        def round_w1(m, copy):
            src = w1_low[:, :, blocks(m, m)] if m < 2 else w1_late[m - 2][:]
            copy(packed(w_bf[1][m]), planar(src))

        def quantise_w(s, m):
            nc.vector.quantize_mx(
                out=w_codes[s][m][:].bitcast(E4M3),
                scales=w_scales[:, s, blocks(m, m)],
                in_=w_bf[s][m].rearrange("p d j -> p (d j)"),
            )

        def multiply(s, m):
            for bank, tok in zip(banks[m], halves):
                nc.tensor.matmul_mx(
                    out=bank[:],
                    lhsT=w_codes[s][m][:].bitcast(E4M3),
                    lhsT_scale=w_scales[:, s, blocks(m, m)],
                    rhs=g_codes[s][:, tok].bitcast(E5M2),
                    rhs_scale=g_scales[s][:, tok],
                    start=(s == 0),
                    stop=(s == PASSES - 1),
                )

        def empty_on_scalar(res, src):
            nc.scalar.activation(res, src, COPY, scale=BETA)

        def empty_on_vector(res, src):
            nc.vector.tensor_scalar_mul(res, src, BETA)

        def store_halves(m):
            for h, tok in enumerate(halves):
                res = keep.tile([P, HALF_T], F32, name="res%d_%d" % (m, h))
                empty_on_scalar(res[:], banks[m][h][:])
                nc.sync.dma_start(out=out[blocks(m, m), tok], in_=res[:])

        def store_whole(m):
            res = keep.tile([P, T], F32, name="res%d" % m)
            empty_on_vector(res[:, first_half], banks[m][0][:])
            empty_on_scalar(res[:, second_half], banks[m][1][:])
            nc.sync.dma_start(out=out[blocks(m, m), :], in_=res[:])

        for j in (0, 2):
            gather_on_scalar(0, j)
            gather_on_vector(0, j + 1)
        for q in range(2):
            subtract(dy0[:, 2 * q : 2 * q + 2, :], picked[0][q], slice(0, T))
        for tok in halves:
            join_z0(tok)
        for tok in halves:
            quantise_g(0, tok)

        gather_on_scalar(1, 0)
        gather_on_vector(1, 1)
        move_book(1, 3)
        gather_on_scalar(1, 2)
        gather_on_scalar(1, 3)
        for q in range(2):
            for tok in halves:
                subtract(dy1[q], picked[1][q], tok)
            for tok in halves:
                join_pair(q, tok)
        for tok in halves:
            weave(tok)
        quantise_g(1, first_half)

        round_w0_low(0, 1, 1)
        round_w0_low(0, 0, 0)
        round_w0_low(1, 1, 0)
        quantise_g(1, slice(HALF_T, HALF_T + T // 4))
        quantise_w(0, 0)
        multiply(0, 0)
        quantise_g(1, slice(HALF_T + T // 4, T))
        quantise_w(0, 1)
        multiply(0, 1)

        round_w1(0, nc.vector.tensor_copy)
        round_w1(1, nc.scalar.copy)
        quantise_w(1, 0)
        multiply(1, 0)
        quantise_w(1, 1)
        multiply(1, 1)
        round_w0_high(2, nc.scalar.copy)
        round_w0_high(3, nc.vector.tensor_copy)
        quantise_w(0, 2)
        multiply(0, 2)
        round_w1(2, nc.vector.tensor_copy)
        quantise_w(0, 3)
        quantise_w(1, 2)
        multiply(1, 2)
        multiply(0, 3)
        round_w1(3, nc.vector.tensor_copy)
        quantise_w(1, 3)
        multiply(1, 3)

        for m in range(BLOCKS - 1):
            store_halves(m)
        store_whole(3)
